import numpy as np
import ml_dtypes


def mxq(x, axis, fmt="e4m3"):
    dtype, down = {"e4m3": (ml_dtypes.float8_e4m3fn, 7), "e5m2": (ml_dtypes.float8_e5m2, 14)}[fmt]
    v = np.moveaxis(np.asarray(x, np.float32).astype(ml_dtypes.bfloat16).astype(np.float64), axis, -1)
    blocks = v.reshape(v.shape[:-1] + (-1, 32))
    amax = np.abs(blocks).max(-1, keepdims=True)
    byte = np.maximum(np.where(amax > 0, np.frexp(amax)[1] - 1 + 127, 0) - down, 1)
    scale = np.exp2(byte - 127.0)
    codes = (blocks / scale).astype(np.float32).astype(dtype).astype(np.float64)
    return np.moveaxis((codes * scale).reshape(v.shape), -1, axis)


WIDE = False


def mx_kscale(k):
    if not WIDE:
        return np.ones(k)
    levels = np.array([10, -10, 5, -5, 0])
    if k % 512:
        return np.exp2(np.random.permutation(np.resize(levels, k // 32))).repeat(32)
    a = np.empty((k // 512, 16))
    for p in range(k // 512):
        a[p, :8] = np.random.permutation(np.resize(levels, 8))
        for g in range(8):
            far = levels[np.abs(levels - a[p, g]) >= 10]
            a[p, g + 8] = far[np.random.randint(len(far))]
    return np.exp2(a.ravel()).repeat(32)


BF16 = ml_dtypes.bfloat16


def bf(x):
    return np.asarray(x, np.float32).astype(BF16)


def f64(x):
    return np.asarray(x).astype(np.float64)


N, V, K, E = 4096, 1024, 512, 512


def topic_proportions(x, wz, bz):
    logits = (mxq(f64(x), 1, "e4m3") @ mxq(f64(wz), 0, "e4m3")) + f64(bz)[None, :]
    e = np.exp(logits - logits.max(axis=1, keepdims=True))
    return e / e.sum(axis=1, keepdims=True)


def draw0():
    s, u, t = mx_kscale(V), mx_kscale(E), mx_kscale(K)
    return {
        "x": bf(np.random.standard_normal((N, V)) * s),
        "wz": bf(np.random.standard_normal((V, K)) / np.sqrt(V) / s[:, None]),
        "bz": bf(0.3 * np.random.standard_normal(K)),
        "g": bf((1.0 + 0.1 * np.random.standard_normal(K)) * t),
        "alpha": bf(np.random.standard_normal((K, E)) * u[None, :] / t[:, None]),
        "rho": bf(np.random.standard_normal((E, V)) / np.sqrt(E) / u[:, None]),
        "m": bf(0.5 * np.random.standard_normal(V)),
    }


def core(x, wz, bz, g, alpha, rho, m):
    n_topics = wz.shape[1]
    n_words = rho.shape[1]
    theta = topic_proportions(x, wz, bz)
    c = (n_topics * theta - 1.0) * f64(g)[None, :]
    eta = mxq(f64(alpha), 1, "e4m3") @ mxq(f64(rho), 0, "e4m3")
    t = (mxq(c, 1, "e4m3") @ mxq(eta, 0, "e4m3")) / np.sqrt(n_topics) + f64(m)[None, :]
    top = t.max(axis=1, keepdims=True)
    log_norm = top + np.log(np.exp(t - top).sum(axis=1, keepdims=True))
    return t - log_norm + np.log(n_words)


def e4m3fn_bytes(y):
    return np.clip(np.asarray(y, np.float64), -448.0, 448.0).astype(np.float32).astype(ml_dtypes.float8_e4m3fn).view(np.uint8)


def e4m3fn_values(b):
    return np.asarray(b, np.uint8).view(ml_dtypes.float8_e4m3fn).astype(np.float64)


def setup_inputs():
    d = draw0()
    x0 = np.asarray(d['x']).astype(np.float64)
    s = (np.max(np.abs(x0), axis=(0,), keepdims=True) / 448.0).astype(np.float32)
    out = {}
    for k, v in d.items():
        if k == 'x':
            out['x_bytes'] = e4m3fn_bytes(x0 / s.astype(np.float64))
            out['x_scale'] = s
        else:
            out[k] = v
    return out


def reference(x_bytes, x_scale, wz, bz, g, alpha, rho, m):
    return core(e4m3fn_values(x_bytes) * x_scale.astype(np.float64), wz, bz, g, alpha, rho, m)

@@ -1,0 +1,518 @@
+import math
+from contextlib import ExitStack
+
+import concourse.mybir as mybir
+from concourse.masks import make_identity
+
+N, V, K, E = 4096, 1024, 512, 512
+FLOPS = 2 * N * V * K + 2 * K * E * V + 2 * N * K * V
+
+F32 = mybir.dt.float32
+BF16 = mybir.dt.bfloat16
+I32 = mybir.dt.int32
+U32 = mybir.dt.uint32
+U8 = mybir.dt.uint8
+FP8 = mybir.dt.float8_e4m3fn
+FP8X4 = mybir.dt.float8_e4m3fn_x4
+ALU = mybir.AluOpType
+ACT = mybir.ActivationFunctionType
+
+P = 128
+PACK = 4
+GROUP_TILES = 2
+GROUP = GROUP_TILES * P
+TILES = N // P
+GROUPS = N // GROUP
+WORD_SLICES = V // P
+BATCH_TILES = 4
+BATCHES = TILES // BATCH_TILES
+PER_BANK = 512 // GROUP
+
+AT_TURN_X = 1
+AT_QUANT_X = GROUP_TILES + 3
+LEAD = 4
+AT_LOGITS = AT_QUANT_X + 1 + LEAD
+AT_MAX1 = AT_LOGITS + GROUP_TILES
+AT_CENTRE = AT_MAX1 + 1
+AT_GAIN = AT_CENTRE + 1
+AT_QUANT_C = AT_GAIN + GROUP_TILES
+AT_WORDS = AT_QUANT_C
+AT_MAX2 = AT_WORDS + GROUP_TILES
+AT_EXP2 = AT_MAX2 + 1
+LOG_BATCHES = [(f, 4) for f in range(0, 28, 4)] + [(28, 2), (30, 2)]
+STEPS = TILES + AT_EXP2 + 1
+ROOT = 512
+PLAIN_L = 0
+PLAIN_T = 0
+PLAIN_C = 0
+STEPPED_CODES = True
+SCALES_IN_PSUM = False
+X_BANK = "mx_bank0" if SCALES_IN_PSUM else "x_bank"
+LOGIT_ACC = "mx_bank1" if SCALES_IN_PSUM else "mx_bank2"
+V_HALF = (34, 35, 36, 37, 38, 39, 40, 41)
+V_FULL = (46, 47, 48)
+V_FINISHES_FROM = 46
+
+
+def tile_sparseadditiveembeddedtopicdecoder_t_kernel(tc, x_bytes, x_scale, wz, bz, g, alpha, rho, m, out):
+    nc = tc.nc
+    with ExitStack() as ctx:
+        keep = ctx.enter_context(tc.tile_pool(name="keep", bufs=1))
+        work = ctx.enter_context(tc.tile_pool(name="work", bufs=2))
+        psum = ctx.enter_context(tc.psum_pool(name="psum", bufs=1))
+        ctx.enter_context(tc.manual_schedule())
+
+        live = {}
+        batch_of = {first + a: (b, a) for b, (first, count) in enumerate(LOG_BATCHES) for a in range(count)}
+        chain_todo = []
+        finish_todo = []
+
+        def bank(tag):
+            return psum.tile([P, 512], F32, name=tag, tag=tag)
+
+        def wide_tile(shape, dtype):
+            return work.tile(shape, dtype, name="wide", tag="wide", bufs=11, align_bytes=64)
+
+        def quantise(codes, scales, grouped):
+            nc.vector.quantize_mx(out=codes.bitcast(FP8X4), scales=scales, in_=grouped)
+
+        def mx_pass(acc, lhs_codes, lhs_scales, rhs_codes, rhs_scales, start, stop):
+            nc.tensor.matmul_mx(
+                out=acc, lhsT=lhs_codes.bitcast(FP8X4), lhsT_scale=lhs_scales,
+                rhs=rhs_codes.bitcast(FP8X4), rhs_scale=rhs_scales, start=start, stop=stop,
+            )
+
+        def turn(dst, src, plain):
+            if plain:
+                nc.tensor.matmul(dst, lhsT=src, rhs=ident[:], start=True, stop=True)
+            else:
+                nc.tensor.transpose(dst, src, ident[:])
+
+        def tile_at(step, offset):
+            i = step - offset
+            return i if 0 <= i < TILES else None
+
+        def group_at(step, offset, size):
+            q, r = divmod(step - offset, size)
+            return q if r == 0 and 0 <= q < TILES // size else None
+
+        def load_x(grp):
+            xb = work.tile([P, BATCH_TILES * V], U8, name="xb", tag="xb", bufs=3)
+            rows = x_bytes[grp * BATCH_TILES * P:(grp + 1) * BATCH_TILES * P, :]
+            nc.sync.dma_start(out=xb[:], in_=rows.rearrange("(p a) v -> p (a v)", a=BATCH_TILES))
+            live["xb", grp] = xb
+
+        scale_cols = keep.tile([P, 2, PACK], F32)
+        nc.sync.dma_start(out=scale_cols[:], in_=x_scale.rearrange("o (h p t) -> p (o h) t", p=P, t=PACK))
+        load_x(0)
+        wz_raw = []
+        for h in range(2):
+            raw = keep.tile([P, PACK, K], BF16, name="wz_raw%d" % h)
+            nc.sync.dma_start(out=raw[:], in_=wz[h * 512:(h + 1) * 512, :].rearrange("(p j) c -> p j c", j=PACK))
+            wz_raw.append(raw)
+        bz_raw = keep.tile([P, PACK], BF16)
+        nc.sync.dma_start(out=bz_raw[:], in_=bz.rearrange("(p t) -> p t", t=PACK))
+        g_raw = keep.tile([P, PACK], BF16)
+        nc.sync.dma_start(out=g_raw[:], in_=g.rearrange("(p t) -> p t", t=PACK))
+        load_x(1)
+        alpha_raw = keep.tile([P, PACK, E], BF16)
+        nc.sync.dma_start(out=alpha_raw[:], in_=alpha.rearrange("(p t) e -> p t e", t=PACK))
+        rho_raw = []
+        for h in range(2):
+            raw = keep.tile([P, PACK, 512], BF16, name="rho_raw%d" % h)
+            nc.sync.dma_start(out=raw[:], in_=rho.rearrange("(p j) v -> p j v", j=PACK)[:, :, h * 512:(h + 1) * 512])
+            rho_raw.append(raw)
+
+        ident = keep.tile([P, P], F32)
+        make_identity(nc, ident[:])
+        m_rows = keep.tile([P, P], BF16)
+        nc.gpsimd.memset(m_rows[:], 0.0)
+        nc.sync.dma_start(out=m_rows[0:WORD_SLICES, :], in_=m.rearrange("(j w) -> j w", w=P))
+
+        x_scales = []
+        scales_sb = None if SCALES_IN_PSUM else keep.tile([P, V], F32, name="scales_sb")
+        for half in range(2):
+            spread = bank(("scale_bank%d" if SCALES_IN_PSUM else "word_bank%d") % half)
+            for q in range(4):
+                if STEPPED_CODES:
+                    h, e = divmod(q, 2)
+                    col = scale_cols[:, h, 2 * half + e:2 * half + e + 1]
+                    dst = spread[:, h * 256 + e:(h + 1) * 256:2]
+                else:
+                    col = scale_cols[:, half, q:q + 1]
+                    dst = spread[:, q:512:4]
+                nc.tensor.transpose(dst, col.to_broadcast([P, P]), ident[:])
+            if SCALES_IN_PSUM:
+                x_scales.append(spread)
+            else:
+                nc.scalar.activation(out=scales_sb[:, half * 512:(half + 1) * 512], in_=spread[:], func=ACT.Copy)
+
+        wz_codes = keep.tile([P, 2, K], U32, align_bytes=64)
+        wz_scales = keep.tile([P, 2, K], U8, align_bytes=64)
+        alpha_codes = keep.tile([P, K], U32, align_bytes=64)
+        alpha_scales = keep.tile([P, K], U8, align_bytes=64)
+        rho_codes = keep.tile([P, V], U32, align_bytes=64)
+        rho_scales = keep.tile([P, V], U8, align_bytes=64)
+        eta_codes = keep.tile([P, V], U32, align_bytes=64)
+        eta_scales = keep.tile([P, V], U8, align_bytes=64)
+        bz_cols = keep.tile([P, PACK], F32)
+        gain_cols = keep.tile([P, PACK], F32)
+        m_rows32 = keep.tile([P, P], F32)
+        m_cols = keep.tile([P, WORD_SLICES], F32)
+        exp_sink = keep.tile([P, V], BF16)
+        root_power = keep.tile([P, BATCH_TILES], F32)
+        nc.gpsimd.memset(root_power[:], 1.0 / ROOT)
+
+        def group_wz(h, copy):
+            grouped = wide_tile([P, K * PACK], BF16)
+            copy(out=grouped[:].rearrange("p (t q j) -> p t q j", t=PACK, j=PACK),
+                 in_=wz_raw[h][:].rearrange("p j (q t) -> p t q j", t=PACK))
+            live["wz", h] = grouped
+
+        def quant_wz(h):
+            quantise(wz_codes[:, h, :], wz_scales[:, h, :], live["wz", h][:])
+
+        def cast_vectors():
+            nc.vector.tensor_scalar(out=bz_cols[:], in0=bz_raw[:], scalar1=-1.0, scalar2=None, op0=ALU.mult)
+            nc.vector.tensor_scalar(out=gain_cols[:], in0=g_raw[:], scalar1=float(K), scalar2=None, op0=ALU.mult)
+
+        def turn_alpha():
+            grouped = wide_tile([P, K * PACK], BF16)
+            pairs = grouped[:].bitcast(F32).rearrange("p (t q u) -> p t q u", t=PACK, u=2)
+            for half, tag in enumerate(("logit_bank", "centre_bank")):
+                turned = bank(tag)
+                for tt in range(2):
+                    words = alpha_raw[:, 2 * half + tt, :].bitcast(F32)
+                    for u in range(2):
+                        q = 2 * tt + u
+                        nc.tensor.transpose(turned[:, q * P:(q + 1) * P], words[:, u:2 * P:2], ident[:])
+                nc.scalar.copy(out=pairs[:, 2 * half:2 * half + 2, :, :],
+                               in_=turned[:].rearrange("p (t u q) -> p t q u", t=2, u=2))
+            live["alpha"] = grouped
+
+        def gp_copy(out, in_):
+            nc.gpsimd.tensor_scalar(out=out, in0=in_, scalar1=1.0, scalar2=0.0, op0=ALU.mult, op1=ALU.add)
+
+        def group_rho(h, part):
+            if part == 0:
+                live["rho", h] = wide_tile([P, 512 * PACK], BF16)
+            nc.scalar.copy(out=live["rho", h][:, part * 1024:(part + 1) * 1024].rearrange("p (c i j) -> p c j i", i=4, j=PACK),
+                           in_=rho_raw[h][:, :, part * 256:(part + 1) * 256].rearrange("p j (c i) -> p c j i", i=4))
+
+        def quant_rho(h):
+            cols = slice(h * 512, (h + 1) * 512)
+            quantise(rho_codes[:, cols], rho_scales[:, cols], live["rho", h][:])
+
+        def turn_m():
+            nc.scalar.copy(out=m_rows32[:], in_=m_rows[:])
+            turned = bank("centre_bank")
+            nc.tensor.transpose(turned[:, 0:P], m_rows32[:], ident[:])
+            nc.scalar.copy(out=m_cols[:], in_=turned[:, 0:WORD_SLICES])
+
+        def eta_mm(j):
+            acc = bank(("logit_bank", "centre_bank")[j % 2] if j in (2, 3) else "word_bank%d" % (j % 2))
+            cols = slice(j * P, (j + 1) * P)
+            for t in range(PACK):
+                topics = slice(t * P, (t + 1) * P)
+                mx_pass(acc[:, topics], alpha_codes[:, topics], alpha_scales[:, topics],
+                        rho_codes[:, cols], rho_scales[:, cols], True, True)
+            live["eta_acc", j] = acc
+
+        def eta_out(j, copy):
+            h, r = divmod(j, 4)
+            if r == 0:
+                live["eta", h] = wide_tile([P, 512 * PACK], BF16)
+            acc = live["eta_acc", j]
+            copy(out=live["eta", h][:, r * 512:(r + 1) * 512].rearrange("p (w t) -> p w t", t=PACK),
+                           in_=acc[:].rearrange("p (t w) -> p w t", t=PACK))
+
+        def quant_eta(h):
+            cols = slice(h * 512, (h + 1) * 512)
+            quantise(eta_codes[:, cols], eta_scales[:, cols], live["eta", h][:])
+
+        def scale_x(i):
+            grp, a = divmod(i, BATCH_TILES)
+            xs = work.tile([P, V], BF16, name="xs", tag="xs", bufs=4)
+            codes = live["xb", grp][:, a * V:(a + 1) * V].bitcast(FP8)
+            if not SCALES_IN_PSUM:
+                nc.vector.tensor_tensor(
+                    out=xs[:].rearrange("n (u q e) -> n u q e", u=2, e=2),
+                    in0=codes.rearrange("n (q u e) -> n u q e", u=2, e=2),
+                    in1=scales_sb[:].rearrange("n (u q e) -> n u q e", u=2, e=2), op=ALU.mult,
+                )
+            for half in range(2 if SCALES_IN_PSUM else 0):
+                cols = slice(half * 512, (half + 1) * 512)
+                if STEPPED_CODES:
+                    nc.vector.tensor_tensor(
+                        out=xs[:, cols].rearrange("n (q e) -> n q e", e=2),
+                        in0=codes.rearrange("n (q u e) -> n u q e", u=2, e=2)[:, half, :, :],
+                        in1=x_scales[half][:].rearrange("n (q e) -> n q e", e=2), op=ALU.mult,
+                    )
+                else:
+                    nc.vector.tensor_tensor(out=xs[:, cols], in0=codes[:, cols], in1=x_scales[half][:], op=ALU.mult)
+            live["xs", i] = xs
+
+        def turn_x(i):
+            grp, a = divmod(i, GROUP_TILES)
+            if a == 0:
+                live["xw", grp] = work.tile([P, 2, GROUP * PACK], BF16, name="xw", tag="xw", bufs=3, align_bytes=64)
+            words = live["xs", i][:].bitcast(F32)
+            turned = bank(X_BANK)
+            for q in range(4):
+                u, h = divmod(q, 2)
+                src = words[:, q * P:(q + 1) * P] if STEPPED_CODES else words[:, h * 256 + u:(h + 1) * 256:2]
+                nc.tensor.transpose(turned[:, q * P:(q + 1) * P], src, ident[:])
+            pairs = live["xw", grp][:].bitcast(F32).rearrange("p h (n u) -> p h n u", u=2)
+            nc.scalar.copy(out=pairs[:, :, a * P:(a + 1) * P, :],
+                           in_=turned[:].rearrange("p (u h n) -> p h n u", u=2, h=2))
+
+        def quant_x(grp):
+            codes = work.tile([P, 2, GROUP], U32, name="x_codes", tag="x_codes", bufs=2 + LEAD // 2, align_bytes=64)
+            scales = work.tile([P, 2, GROUP], U8, name="x_mx_scales", tag="x_mx_scales", bufs=2 + LEAD // 2, align_bytes=64)
+            quantise(codes[:].rearrange("p h n -> p (h n)"), scales[:].rearrange("p h n -> p (h n)"),
+                     live["xw", grp][:].rearrange("p h n -> p (h n)"))
+            live["xq", grp] = (codes, scales)
+
+        def logits_mm(i):
+            grp, a = divmod(i, GROUP_TILES)
+            acc = bank(LOGIT_ACC)
+            codes, scales = live["xq", grp]
+            for r in range(PER_BANK):
+                t = a * PER_BANK + r
+                topics = slice(t * P, (t + 1) * P)
+                for h in range(2):
+                    mx_pass(acc[:, r * GROUP:(r + 1) * GROUP], wz_codes[:, h, topics], wz_scales[:, h, topics],
+                            codes[:, h, :], scales[:, h, :], h == 0, h == 1)
+            live["logit_acc"] = acc
+
+        def logits_out(i):
+            grp, a = divmod(i, GROUP_TILES)
+            for r in range(PER_BANK):
+                t = a * PER_BANK + r
+                lt = work.tile([P, GROUP], F32, name="lt", tag="lt", bufs=8)
+                nc.scalar.activation(out=lt[:], in_=live["logit_acc"][:, r * GROUP:(r + 1) * GROUP], func=ACT.Identity,
+                                     scale=-1.0, bias=bz_cols[:, t:t + 1])
+                live["lt", grp, t] = lt
+
+        def max1(i):
+            grp, a = divmod(i, GROUP_TILES)
+            turned = bank("logit_bank")
+            for t in range(PACK):
+                turn(turned[:, t * P:(t + 1) * P], live["lt", grp, t][:, a * P:(a + 1) * P], t < PLAIN_L)
+            live["turned1"] = turned
+
+        def max1_reduce(i):
+            turned = live["turned1"]
+            low = work.tile([P, 1], F32, name="neg_max1", tag="neg_max1", bufs=3)
+            nc.vector.tensor_reduce(out=low[:], in_=turned[:], axis=mybir.AxisListType.X, op=ALU.min)
+            live["neg1", i] = (turned, low)
+
+        def exp1(i):
+            neg, low = live["neg1", i]
+            e1 = work.tile([P, K], F32, name="e1", tag="e1", bufs=3)
+            total = work.tile([P, 1], F32, name="sum1", tag="sum1", bufs=3)
+            nc.scalar.activation(out=e1[:], in_=neg[:], func=ACT.Exp, scale=-1.0, bias=low[:], accum_out=total[:])
+            live["e1", i] = (e1, total)
+
+        def invert(i):
+            inv = work.tile([P, 1], F32, name="inv1", tag="inv1", bufs=3)
+            nc.vector.reciprocal(out=inv[:], in_=live["e1", i][1][:])
+            live["inv", i] = inv
+
+        def centre(i):
+            d = work.tile([P, K], F32, name="centred", tag="centred", bufs=3)
+            nc.gpsimd.tensor_scalar(out=d[:], in0=live["e1", i][0][:], scalar1=live["inv", i][:], scalar2=-1.0 / K,
+                                    op0=ALU.mult, op1=ALU.add)
+            live["d", i] = d
+
+        def gain(i):
+            grp, a = divmod(i, GROUP_TILES)
+            if a == 0:
+                live["cb", grp] = work.tile([P, GROUP * PACK], BF16, name="cb", tag="cb", bufs=2, align_bytes=64)
+            turned = bank("centre_bank")
+            for t in range(PACK):
+                turn(turned[:, t * P:(t + 1) * P], live["d", i][:, t * P:(t + 1) * P], t >= PACK - PLAIN_C)
+            nc.vector.tensor_tensor(
+                out=live["cb", grp][:, a * 512:(a + 1) * 512].rearrange("p (n t) -> p n t", t=PACK),
+                in0=turned[:].rearrange("p (t n) -> p n t", t=PACK),
+                in1=gain_cols[:].unsqueeze(1).to_broadcast([P, P, PACK]), op=ALU.mult,
+            )
+
+        def quant_c(grp):
+            codes = work.tile([P, GROUP], U32, name="c_codes", tag="c_codes", bufs=2, align_bytes=64)
+            scales = work.tile([P, GROUP], U8, name="c_mx_scales", tag="c_mx_scales", bufs=2, align_bytes=64)
+            quantise(codes[:], scales[:], live["cb", grp][:])
+            live["cq", grp] = (codes, scales)
+
+        def words_mm(i, b):
+            grp, a = divmod(i, GROUP_TILES)
+            acc = bank("mx_bank%d" % b)
+            codes, scales = live["cq", grp]
+            for r in range(PER_BANK):
+                j = (2 * a + b) * PER_BANK + r
+                cols = slice(j * P, (j + 1) * P)
+                mx_pass(acc[:, r * GROUP:(r + 1) * GROUP], eta_codes[:, cols], eta_scales[:, cols], codes[:], scales[:], True, True)
+            live["word_acc", b] = acc
+
+        def words_out(i, b, on_vector):
+            grp, a = divmod(i, GROUP_TILES)
+            for r in range(PER_BANK):
+                j = (2 * a + b) * PER_BANK + r
+                tt = work.tile([P, GROUP], F32, name="tt", tag="tt", bufs=16)
+                acc = live["word_acc", b][:, r * GROUP:(r + 1) * GROUP]
+                if r < on_vector:
+                    nc.vector.tensor_scalar(out=tt[:], in0=acc, scalar1=1.0 / math.sqrt(K),
+                                            scalar2=m_cols[:, j:j + 1], op0=ALU.mult, op1=ALU.add)
+                else:
+                    nc.scalar.activation(out=tt[:], in_=acc, func=ACT.Identity,
+                                         scale=1.0 / math.sqrt(K), bias=m_cols[:, j:j + 1])
+                live["tt", grp, j] = tt
+
+        def max2_turn(i, half):
+            grp, a = divmod(i, GROUP_TILES)
+            turned = bank("word_bank%d" % half)
+            for r in range(4):
+                turn(turned[:, r * P:(r + 1) * P], live["tt", grp, 4 * half + r][:, a * P:(a + 1) * P], half == 1 and r < PLAIN_T)
+            live["turned2", half] = turned
+
+        def max2(i, half):
+            grp, a = batch_of[i]
+            if half == 0:
+                live["neg2", i] = wide_tile([P, V], F32)
+                live["low_half", i] = work.tile([P, 1], F32, name="low_half", tag="low_half", bufs=2)
+                if a == 0:
+                    live["low2", grp] = work.tile([P, LOG_BATCHES[grp][1]], F32, name="neg_max2", tag="neg_max2", bufs=4)
+            turned = live["turned2", half]
+            nc.vector.tensor_scalar(
+                out=live["neg2", i][:, half * 512:(half + 1) * 512], in0=turned[:], scalar1=-1.0,
+                scalar2=None if half == 0 else live["low_half", i][:], op0=ALU.mult, op1=ALU.min,
+                accum_out=live["low_half", i][:] if half == 0 else live["low2", grp][:, a:a + 1],
+            )
+
+        def exp2(i):
+            grp, a = batch_of[i]
+            if a == 0:
+                live["sum2", grp] = work.tile([P, LOG_BATCHES[grp][1]], F32, name="sum2", tag="sum2", bufs=3)
+            nc.scalar.activation(out=exp_sink[:], in_=live["neg2", i][:], func=ACT.Exp, scale=-1.0,
+                                 bias=live["low2", grp][:, a:a + 1], accum_out=live["sum2", grp][:, a:a + 1])
+
+        def small(key, grp):
+            t = work.tile([P, LOG_BATCHES[grp][1]], F32, name=key, tag=key, bufs=3)
+            live[key, grp] = t
+            return t[:]
+
+        def log_root(grp):
+            nc.gpsimd.tensor_tensor(out=small("root", grp), in0=live["sum2", grp][:], in1=root_power[:, 0:LOG_BATCHES[grp][1]], op=ALU.pow)
+
+        def log_rest(grp):
+            nc.vector.tensor_scalar(out=small("rest", grp), in0=live["root", grp][:], scalar1=float(V) ** (-1.0 / ROOT),
+                                    scalar2=-1.0, op0=ALU.mult, op1=ALU.add)
+            live["series", grp] = live["rest", grp]
+
+        def log_term(grp, c):
+            prev = live["series", grp]
+            nxt = work.tile([P, LOG_BATCHES[grp][1]], F32, name="series", tag="series", bufs=2)
+            nc.vector.scalar_tensor_tensor(out=nxt[:], in0=prev[:], scalar=c, in1=live["rest", grp][:], op0=ALU.add, op1=ALU.mult)
+            live["series", grp] = nxt
+
+        def log_shift(grp):
+            nc.vector.scalar_tensor_tensor(out=small("shift", grp), in0=live["series", grp][:], scalar=-ROOT / 5.0,
+                                           in1=live["low2", grp][:], op0=ALU.mult, op1=ALU.add)
+
+        log_chain = [log_rest, lambda q: log_term(q, -5.0 / 4), lambda q: log_term(q, 5.0 / 3),
+                     lambda q: log_term(q, -5.0 / 2), lambda q: log_term(q, 5.0), log_shift]
+
+        def after_exp2(i):
+            b, a = batch_of[i]
+            if a == LOG_BATCHES[b][1] - 1:
+                log_root(b)
+                chain_todo.extend((b, link) for link in range(len(log_chain)))
+
+        def log_slot():
+            if chain_todo:
+                b, link = chain_todo.pop(0)
+                log_chain[link](b)
+                if link == len(log_chain) - 1:
+                    finish_todo.extend(range(LOG_BATCHES[b][0], LOG_BATCHES[b][0] + LOG_BATCHES[b][1]))
+
+        def finish_slot(engine):
+            if finish_todo:
+                finish(finish_todo.pop(0), engine)
+
+        def finish(i, engine):
+            grp, a = batch_of[i]
+            neg = live["neg2", i]
+            engine.tensor_scalar(out=neg[:], in0=neg[:], scalar1=-1.0, scalar2=live["shift", grp][:, a:a + 1],
+                                    op0=ALU.mult, op1=ALU.add)
+            grp, a = divmod(i, BATCH_TILES)
+            rows = out[grp * BATCH_TILES * P:(grp + 1) * BATCH_TILES * P, :].rearrange("(p a) v -> p a v", a=BATCH_TILES)
+            nc.sync.dma_start(out=rows[:, a, :], in_=neg[:])
+
+        vector_setup = {
+            2: cast_vectors, 4: lambda: quant_wz(0), 3: lambda: quant_wz(1),
+            6: lambda: quantise(alpha_codes[:], alpha_scales[:], live["alpha"][:]),
+            7: lambda: quant_rho(0), 8: lambda: quant_rho(1), 12: lambda: quant_eta(0), 16: lambda: quant_eta(1),
+        }
+        scalar_setup = {0: lambda: (group_wz(0, nc.scalar.copy), group_wz(1, gp_copy)), 2: turn_alpha,
+                        3: lambda: group_rho(0, 0), 4: lambda: group_rho(0, 1), 5: lambda: group_rho(1, 0),
+                        6: lambda: group_rho(1, 1), 7: turn_m}
+        tensor_setup = {8: (0, 1), 9: (2, 3), 10: (4,), 11: (5,), 12: (6,), 13: (7,)}
+
+        def on_tile(step, offset, stage):
+            i = tile_at(step, offset)
+            if i is not None:
+                stage(i)
+
+        def on_group(step, offset, stage, size=GROUP_TILES):
+            q = group_at(step, offset, size)
+            if q is not None:
+                stage(q)
+
+        for step in range(STEPS):
+            tail = step >= V_FINISHES_FROM
+            if step % BATCH_TILES == 0 and step // BATCH_TILES + 2 < BATCHES:
+                load_x(step // BATCH_TILES + 2)
+            on_tile(step, AT_WORDS + 1, lambda i: words_out(i, 1, 2 if step in V_FULL else 1 if step in V_HALF else 0))
+            for j in tensor_setup.get(step - 1, ()):
+                eta_out(j, nc.scalar.copy)
+            on_tile(step, AT_MAX2, lambda i: max2_turn(i, 0))
+            on_tile(step, AT_EXP2, exp2)
+            on_tile(step, AT_TURN_X, turn_x)
+            on_tile(step, 0, scale_x)
+            log_slot()
+            if step in vector_setup:
+                vector_setup[step]()
+            on_group(step, AT_QUANT_X, quant_x)
+            on_group(step, AT_QUANT_C, quant_c)
+            if tail:
+                finish_slot(nc.vector)
+            log_slot()
+            on_tile(step, AT_CENTRE, invert)
+            on_tile(step, AT_CENTRE, centre)
+            if not tail:
+                finish_slot(nc.gpsimd)
+            on_tile(step, AT_MAX2, lambda i: max2(i, 0))
+            if tail:
+                log_slot()
+            on_tile(step, AT_LOGITS, logits_mm)
+            on_tile(step, AT_MAX1, max1)
+            on_tile(step, AT_EXP2, after_exp2)
+            on_tile(step, AT_LOGITS, logits_out)
+            on_tile(step, AT_MAX1, max1_reduce)
+            on_tile(step, AT_MAX2, lambda i: max2_turn(i, 1))
+            on_tile(step, AT_MAX2, lambda i: max2(i, 1))
+            if tail:
+                log_slot()
+                finish_slot(nc.vector)
+            on_tile(step, AT_MAX1, exp1)
+            on_tile(step, AT_GAIN, gain)
+            on_tile(step, AT_WORDS, lambda i: words_mm(i, 0))
+            on_tile(step, AT_WORDS, lambda i: words_mm(i, 1))
+            on_tile(step, AT_WORDS, lambda i: words_out(i, 0, 0))
+            for j in tensor_setup.get(step, ()):
+                eta_mm(j)
+            if step in scalar_setup:
+                scalar_setup[step]()
+        while chain_todo or finish_todo:
+            log_slot()
+            finish_slot(nc.vector)

@@ -39,19 +39,20 @@ AT_QUANT_C = AT_GAIN + GROUP_TILES
 AT_WORDS = AT_QUANT_C
 AT_MAX2 = AT_WORDS + GROUP_TILES
 AT_EXP2 = AT_MAX2 + 1
-LOG_BATCHES = [(f, 4) for f in range(0, 28, 4)] + [(28, 2), (30, 2)]
+SMALL_FROM = 28
+DIAG_TILES = 20
+LOG_BATCHES = [(f, 4) for f in range(0, SMALL_FROM, 4)] + [(f, 2) for f in range(SMALL_FROM, TILES, 2)]
 STEPS = TILES + AT_EXP2 + 1
 ROOT = 512
+ETA_STEPS = {8: (0, 1), 9: (2, 3), 10: (4,), 11: (5,), 12: (6,), 13: (7,)}
 PLAIN_L = 0
 PLAIN_T = 0
-PLAIN_C = 0
-STEPPED_CODES = True
-SCALES_IN_PSUM = False
-X_BANK = "mx_bank0" if SCALES_IN_PSUM else "x_bank"
-LOGIT_ACC = "mx_bank1" if SCALES_IN_PSUM else "mx_bank2"
+PLAIN_C = 1
 V_HALF = (34, 35, 36, 37, 38, 39, 40, 41)
 V_FULL = (46, 47, 48)
-V_FINISHES_FROM = 46
+ETA_ON_V = (1, 3)
+TAIL = 45
+S_FINISHES = (47, 48, 49, 50)
 
 
 def tile_sparseadditiveembeddedtopicdecoder_t_kernel(tc, x_bytes, x_scale, wz, bz, g, alpha, rho, m, out):
@@ -64,6 +65,7 @@ def tile_sparseadditiveembeddedtopicdecoder_t_kernel(tc, x_bytes, x_scale, wz, b
 
         live = {}
         batch_of = {first + a: (b, a) for b, (first, count) in enumerate(LOG_BATCHES) for a in range(count)}
+        root_steps = [AT_EXP2 + first + count - 1 for first, count in LOG_BATCHES]
         chain_todo = []
         finish_todo = []
 
@@ -104,9 +106,10 @@ def tile_sparseadditiveembeddedtopicdecoder_t_kernel(tc, x_bytes, x_scale, wz, b
 
         scale_cols = keep.tile([P, 2, PACK], F32)
         nc.sync.dma_start(out=scale_cols[:], in_=x_scale.rearrange("o (h p t) -> p (o h) t", p=P, t=PACK))
-        load_x(0)
         wz_raw = []
         for h in range(2):
+            if h == 1:
+                load_x(0)
             raw = keep.tile([P, PACK, K], BF16, name="wz_raw%d" % h)
             nc.sync.dma_start(out=raw[:], in_=wz[h * 512:(h + 1) * 512, :].rearrange("(p j) c -> p j c", j=PACK))
             wz_raw.append(raw)
@@ -129,23 +132,17 @@ def tile_sparseadditiveembeddedtopicdecoder_t_kernel(tc, x_bytes, x_scale, wz, b
         nc.gpsimd.memset(m_rows[:], 0.0)
         nc.sync.dma_start(out=m_rows[0:WORD_SLICES, :], in_=m.rearrange("(j w) -> j w", w=P))
 
-        x_scales = []
-        scales_sb = None if SCALES_IN_PSUM else keep.tile([P, V], F32, name="scales_sb")
-        for half in range(2):
-            spread = bank(("scale_bank%d" if SCALES_IN_PSUM else "word_bank%d") % half)
+        x_scales = keep.tile([P, V], F32)
+        for u in range(2):
+            spread = bank("word_bank%d" % u)
             for q in range(4):
-                if STEPPED_CODES:
-                    h, e = divmod(q, 2)
-                    col = scale_cols[:, h, 2 * half + e:2 * half + e + 1]
-                    dst = spread[:, h * 256 + e:(h + 1) * 256:2]
-                else:
-                    col = scale_cols[:, half, q:q + 1]
-                    dst = spread[:, q:512:4]
-                nc.tensor.transpose(dst, col.to_broadcast([P, P]), ident[:])
-            if SCALES_IN_PSUM:
-                x_scales.append(spread)
-            else:
-                nc.scalar.activation(out=scales_sb[:, half * 512:(half + 1) * 512], in_=spread[:], func=ACT.Copy)
+                h, e = divmod(q, 2)
+                col = scale_cols[:, h, 2 * u + e:2 * u + e + 1].to_broadcast([P, P])
+                nc.tensor.transpose(spread[:, q * P:(q + 1) * P], col, ident[:])
+            nc.scalar.activation(
+                out=x_scales[:, u * 512:(u + 1) * 512].rearrange("n (h p e) -> n h p e", h=2, e=2),
+                in_=spread[:].rearrange("n (h e p) -> n h p e", h=2, e=2), func=ACT.Copy,
+            )
 
         wz_codes = keep.tile([P, 2, K], U32, align_bytes=64)
         wz_scales = keep.tile([P, 2, K], U8, align_bytes=64)
@@ -163,11 +160,12 @@ def tile_sparseadditiveembeddedtopicdecoder_t_kernel(tc, x_bytes, x_scale, wz, b
         root_power = keep.tile([P, BATCH_TILES], F32)
         nc.gpsimd.memset(root_power[:], 1.0 / ROOT)
 
-        def group_wz(h, copy):
-            grouped = wide_tile([P, K * PACK], BF16)
-            copy(out=grouped[:].rearrange("p (t q j) -> p t q j", t=PACK, j=PACK),
-                 in_=wz_raw[h][:].rearrange("p j (q t) -> p t q j", t=PACK))
-            live["wz", h] = grouped
+        def group_wz(h, part, copy):
+            if part == 0:
+                live["wz", h] = wide_tile([P, K * PACK], BF16)
+            slots = slice(2 * part, 2 * part + 2)
+            copy(out=live["wz", h][:].rearrange("p (t q j) -> p t q j", t=PACK, j=PACK)[:, slots],
+                           in_=wz_raw[h][:].rearrange("p j (q t) -> p t q j", t=PACK)[:, slots])
 
         def quant_wz(h):
             quantise(wz_codes[:, h, :], wz_scales[:, h, :], live["wz", h][:])
@@ -189,9 +187,6 @@ def tile_sparseadditiveembeddedtopicdecoder_t_kernel(tc, x_bytes, x_scale, wz, b
                 nc.scalar.copy(out=pairs[:, 2 * half:2 * half + 2, :, :],
                                in_=turned[:].rearrange("p (t u q) -> p t q u", t=2, u=2))
             live["alpha"] = grouped
-
-        def gp_copy(out, in_):
-            nc.gpsimd.tensor_scalar(out=out, in0=in_, scalar1=1.0, scalar2=0.0, op0=ALU.mult, op1=ALU.add)
 
         def group_rho(h, part):
             if part == 0:
@@ -220,7 +215,7 @@ def tile_sparseadditiveembeddedtopicdecoder_t_kernel(tc, x_bytes, x_scale, wz, b
 
         def eta_out(j, copy):
             h, r = divmod(j, 4)
-            if r == 0:
+            if ("eta", h) not in live:
                 live["eta", h] = wide_tile([P, 512 * PACK], BF16)
             acc = live["eta_acc", j]
             copy(out=live["eta", h][:, r * 512:(r + 1) * 512].rearrange("p (w t) -> p w t", t=PACK),
@@ -234,22 +229,11 @@ def tile_sparseadditiveembeddedtopicdecoder_t_kernel(tc, x_bytes, x_scale, wz, b
             grp, a = divmod(i, BATCH_TILES)
             xs = work.tile([P, V], BF16, name="xs", tag="xs", bufs=4)
             codes = live["xb", grp][:, a * V:(a + 1) * V].bitcast(FP8)
-            if not SCALES_IN_PSUM:
-                nc.vector.tensor_tensor(
-                    out=xs[:].rearrange("n (u q e) -> n u q e", u=2, e=2),
-                    in0=codes.rearrange("n (q u e) -> n u q e", u=2, e=2),
-                    in1=scales_sb[:].rearrange("n (u q e) -> n u q e", u=2, e=2), op=ALU.mult,
-                )
-            for half in range(2 if SCALES_IN_PSUM else 0):
-                cols = slice(half * 512, (half + 1) * 512)
-                if STEPPED_CODES:
-                    nc.vector.tensor_tensor(
-                        out=xs[:, cols].rearrange("n (q e) -> n q e", e=2),
-                        in0=codes.rearrange("n (q u e) -> n u q e", u=2, e=2)[:, half, :, :],
-                        in1=x_scales[half][:].rearrange("n (q e) -> n q e", e=2), op=ALU.mult,
-                    )
-                else:
-                    nc.vector.tensor_tensor(out=xs[:, cols], in0=codes[:, cols], in1=x_scales[half][:], op=ALU.mult)
+            nc.vector.tensor_tensor(
+                out=xs[:].rearrange("n (u q e) -> n u q e", u=2, e=2),
+                in0=codes.rearrange("n (q u e) -> n u q e", u=2, e=2),
+                in1=x_scales[:].rearrange("n (u q e) -> n u q e", u=2, e=2), op=ALU.mult,
+            )
             live["xs", i] = xs
 
         def turn_x(i):
@@ -257,11 +241,9 @@ def tile_sparseadditiveembeddedtopicdecoder_t_kernel(tc, x_bytes, x_scale, wz, b
             if a == 0:
                 live["xw", grp] = work.tile([P, 2, GROUP * PACK], BF16, name="xw", tag="xw", bufs=3, align_bytes=64)
             words = live["xs", i][:].bitcast(F32)
-            turned = bank(X_BANK)
+            turned = bank("x_bank")
             for q in range(4):
-                u, h = divmod(q, 2)
-                src = words[:, q * P:(q + 1) * P] if STEPPED_CODES else words[:, h * 256 + u:(h + 1) * 256:2]
-                nc.tensor.transpose(turned[:, q * P:(q + 1) * P], src, ident[:])
+                nc.tensor.transpose(turned[:, q * P:(q + 1) * P], words[:, q * P:(q + 1) * P], ident[:])
             pairs = live["xw", grp][:].bitcast(F32).rearrange("p h (n u) -> p h n u", u=2)
             nc.scalar.copy(out=pairs[:, :, a * P:(a + 1) * P, :],
                            in_=turned[:].rearrange("p (u h n) -> p h n u", u=2, h=2))
@@ -275,7 +257,7 @@ def tile_sparseadditiveembeddedtopicdecoder_t_kernel(tc, x_bytes, x_scale, wz, b
 
         def logits_mm(i):
             grp, a = divmod(i, GROUP_TILES)
-            acc = bank(LOGIT_ACC)
+            acc = bank("mx_bank2")
             codes, scales = live["xq", grp]
             for r in range(PER_BANK):
                 t = a * PER_BANK + r
@@ -309,7 +291,7 @@ def tile_sparseadditiveembeddedtopicdecoder_t_kernel(tc, x_bytes, x_scale, wz, b
 
         def exp1(i):
             neg, low = live["neg1", i]
-            e1 = work.tile([P, K], F32, name="e1", tag="e1", bufs=3)
+            e1 = work.tile([P, K], F32, name="e1", tag="e1", bufs=4)
             total = work.tile([P, 1], F32, name="sum1", tag="sum1", bufs=3)
             nc.scalar.activation(out=e1[:], in_=neg[:], func=ACT.Exp, scale=-1.0, bias=low[:], accum_out=total[:])
             live["e1", i] = (e1, total)
@@ -320,9 +302,13 @@ def tile_sparseadditiveembeddedtopicdecoder_t_kernel(tc, x_bytes, x_scale, wz, b
             live["inv", i] = inv
 
         def centre(i):
-            d = work.tile([P, K], F32, name="centred", tag="centred", bufs=3)
-            nc.gpsimd.tensor_scalar(out=d[:], in0=live["e1", i][0][:], scalar1=live["inv", i][:], scalar2=-1.0 / K,
-                                    op0=ALU.mult, op1=ALU.add)
+            if i < DIAG_TILES:
+                d = work.tile([P, P], F32, name="inv_diag", tag="inv_diag", bufs=3)
+                nc.gpsimd.tensor_scalar(out=d[:], in0=ident[:], scalar1=live["inv", i][:], scalar2=1.0, op0=ALU.mult, op1=ALU.mult)
+            else:
+                d = work.tile([P, K], F32, name="centred", tag="centred", bufs=3)
+                nc.gpsimd.tensor_scalar(out=d[:], in0=live["e1", i][0][:], scalar1=live["inv", i][:], scalar2=1.0,
+                                        op0=ALU.mult, op1=ALU.mult)
             live["d", i] = d
 
         def gain(i):
@@ -331,11 +317,15 @@ def tile_sparseadditiveembeddedtopicdecoder_t_kernel(tc, x_bytes, x_scale, wz, b
                 live["cb", grp] = work.tile([P, GROUP * PACK], BF16, name="cb", tag="cb", bufs=2, align_bytes=64)
             turned = bank("centre_bank")
             for t in range(PACK):
-                turn(turned[:, t * P:(t + 1) * P], live["d", i][:, t * P:(t + 1) * P], t >= PACK - PLAIN_C)
-            nc.vector.tensor_tensor(
+                if i < DIAG_TILES:
+                    nc.tensor.matmul(turned[:, t * P:(t + 1) * P], lhsT=live["e1", i][0][:, t * P:(t + 1) * P], rhs=live["d", i][:],
+                                     start=True, stop=True)
+                else:
+                    turn(turned[:, t * P:(t + 1) * P], live["d", i][:, t * P:(t + 1) * P], t >= PACK - PLAIN_C)
+            nc.vector.scalar_tensor_tensor(
                 out=live["cb", grp][:, a * 512:(a + 1) * 512].rearrange("p (n t) -> p n t", t=PACK),
-                in0=turned[:].rearrange("p (t n) -> p n t", t=PACK),
-                in1=gain_cols[:].unsqueeze(1).to_broadcast([P, P, PACK]), op=ALU.mult,
+                in0=turned[:].rearrange("p (t n) -> p n t", t=PACK), scalar=-1.0 / K,
+                in1=gain_cols[:].unsqueeze(1).to_broadcast([P, P, PACK]), op0=ALU.add, op1=ALU.mult,
             )
 
         def quant_c(grp):
@@ -435,28 +425,37 @@ def tile_sparseadditiveembeddedtopicdecoder_t_kernel(tc, x_bytes, x_scale, wz, b
                 if link == len(log_chain) - 1:
                     finish_todo.extend(range(LOG_BATCHES[b][0], LOG_BATCHES[b][0] + LOG_BATCHES[b][1]))
 
-        def finish_slot(engine):
+        def finish_slot(*engines):
             if finish_todo:
-                finish(finish_todo.pop(0), engine)
+                finish(finish_todo.pop(0), engines)
 
-        def finish(i, engine):
+        def finish(i, engines):
             grp, a = batch_of[i]
             neg = live["neg2", i]
-            engine.tensor_scalar(out=neg[:], in0=neg[:], scalar1=-1.0, scalar2=live["shift", grp][:, a:a + 1],
-                                    op0=ALU.mult, op1=ALU.add)
+            shift = live["shift", grp][:, a:a + 1]
+            width = V // len(engines)
+            for n, engine in enumerate(engines):
+                part = neg[:, n * width:(n + 1) * width]
+                if engine == "scalar":
+                    nc.scalar.activation(out=part, in_=part, func=ACT.Identity, scale=-1.0, bias=shift)
+                else:
+                    queue = nc.vector if engine == "vector" else nc.gpsimd
+                    queue.tensor_scalar(out=part, in0=part, scalar1=-1.0, scalar2=shift, op0=ALU.mult, op1=ALU.add)
             grp, a = divmod(i, BATCH_TILES)
             rows = out[grp * BATCH_TILES * P:(grp + 1) * BATCH_TILES * P, :].rearrange("(p a) v -> p a v", a=BATCH_TILES)
             nc.sync.dma_start(out=rows[:, a, :], in_=neg[:])
 
         vector_setup = {
-            2: cast_vectors, 4: lambda: quant_wz(0), 3: lambda: quant_wz(1),
-            6: lambda: quantise(alpha_codes[:], alpha_scales[:], live["alpha"][:]),
-            7: lambda: quant_rho(0), 8: lambda: quant_rho(1), 12: lambda: quant_eta(0), 16: lambda: quant_eta(1),
+            1: cast_vectors, 2: lambda: quant_wz(0), 3: lambda: quant_wz(1),
+            4: lambda: quantise(alpha_codes[:], alpha_scales[:], live["alpha"][:]),
+            6: lambda: quant_rho(0), 8: lambda: quant_rho(1), AT_WORDS - 4: lambda: quant_eta(0), AT_WORDS: lambda: quant_eta(1),
         }
-        scalar_setup = {0: lambda: (group_wz(0, nc.scalar.copy), group_wz(1, gp_copy)), 2: turn_alpha,
+        scalar_setup = {0: lambda: group_wz(1, 0, nc.scalar.copy), 1: lambda: group_wz(1, 1, nc.scalar.copy), 2: turn_alpha,
                         3: lambda: group_rho(0, 0), 4: lambda: group_rho(0, 1), 5: lambda: group_rho(1, 0),
                         6: lambda: group_rho(1, 1), 7: turn_m}
-        tensor_setup = {8: (0, 1), 9: (2, 3), 10: (4,), 11: (5,), 12: (6,), 13: (7,)}
+        tensor_setup = ETA_STEPS
+        group_wz(0, 0, nc.vector.tensor_copy)
+        group_wz(0, 1, nc.vector.tensor_copy)
 
         def on_tile(step, offset, stage):
             i = tile_at(step, offset)
@@ -469,12 +468,14 @@ def tile_sparseadditiveembeddedtopicdecoder_t_kernel(tc, x_bytes, x_scale, wz, b
                 stage(q)
 
         for step in range(STEPS):
-            tail = step >= V_FINISHES_FROM
+            drain = step >= TILES
+            tail = step >= TAIL
             if step % BATCH_TILES == 0 and step // BATCH_TILES + 2 < BATCHES:
                 load_x(step // BATCH_TILES + 2)
             on_tile(step, AT_WORDS + 1, lambda i: words_out(i, 1, 2 if step in V_FULL else 1 if step in V_HALF else 0))
             for j in tensor_setup.get(step - 1, ()):
-                eta_out(j, nc.scalar.copy)
+                if j not in ETA_ON_V:
+                    eta_out(j, nc.scalar.copy)
             on_tile(step, AT_MAX2, lambda i: max2_turn(i, 0))
             on_tile(step, AT_EXP2, exp2)
             on_tile(step, AT_TURN_X, turn_x)
@@ -484,26 +485,32 @@ def tile_sparseadditiveembeddedtopicdecoder_t_kernel(tc, x_bytes, x_scale, wz, b
                 vector_setup[step]()
             on_group(step, AT_QUANT_X, quant_x)
             on_group(step, AT_QUANT_C, quant_c)
-            if tail:
-                finish_slot(nc.vector)
+            root_step = step in root_steps
+            if root_step and not tail:
+                finish_slot("vector", "scalar") if not drain else finish_slot("vector")
             log_slot()
             on_tile(step, AT_CENTRE, invert)
             on_tile(step, AT_CENTRE, centre)
-            if not tail:
-                finish_slot(nc.gpsimd)
+            if not root_step and not tail:
+                finish_slot("gpsimd")
+            on_tile(step, AT_EXP2, after_exp2)
+            for j in tensor_setup.get(step - 1, ()):
+                if j in ETA_ON_V:
+                    eta_out(j, nc.vector.tensor_copy)
             on_tile(step, AT_MAX2, lambda i: max2(i, 0))
             if tail:
                 log_slot()
             on_tile(step, AT_LOGITS, logits_mm)
             on_tile(step, AT_MAX1, max1)
-            on_tile(step, AT_EXP2, after_exp2)
             on_tile(step, AT_LOGITS, logits_out)
             on_tile(step, AT_MAX1, max1_reduce)
             on_tile(step, AT_MAX2, lambda i: max2_turn(i, 1))
             on_tile(step, AT_MAX2, lambda i: max2(i, 1))
             if tail:
                 log_slot()
-                finish_slot(nc.vector)
+                finish_slot("vector")
+            if step in S_FINISHES:
+                finish_slot("scalar")
             on_tile(step, AT_MAX1, exp1)
             on_tile(step, AT_GAIN, gain)
             on_tile(step, AT_WORDS, lambda i: words_mm(i, 0))
@@ -515,4 +522,4 @@ def tile_sparseadditiveembeddedtopicdecoder_t_kernel(tc, x_bytes, x_scale, wz, b
                 scalar_setup[step]()
         while chain_todo or finish_todo:
             log_slot()
-            finish_slot(nc.vector)
+            finish_slot("vector")

@@ -39,11 +39,11 @@ AT_QUANT_C = AT_GAIN + GROUP_TILES
 AT_WORDS = AT_QUANT_C
 AT_MAX2 = AT_WORDS + GROUP_TILES
 AT_EXP2 = AT_MAX2 + 1
-SMALL_FROM = 28
+SMALL_FROM = 20
 DIAG_TILES = 20
 LOG_BATCHES = [(f, 4) for f in range(0, SMALL_FROM, 4)] + [(f, 2) for f in range(SMALL_FROM, TILES, 2)]
 STEPS = TILES + AT_EXP2 + 1
-ROOT = 512
+ROOT = 1024
 ETA_STEPS = {8: (0, 1), 9: (2, 3), 10: (4,), 11: (5,), 12: (6,), 13: (7,)}
 PLAIN_L = 0
 PLAIN_T = 0
@@ -51,8 +51,8 @@ PLAIN_C = 1
 V_HALF = (34, 35, 36, 37, 38, 39, 40, 41)
 V_FULL = (46, 47, 48)
 ETA_ON_V = (1, 3)
-TAIL = 45
-S_FINISHES = (47, 48, 49, 50)
+CATCH_UP = (42, 43)
+G_LAST = 48
 
 
 def tile_sparseadditiveembeddedtopicdecoder_t_kernel(tc, x_bytes, x_scale, wz, bz, g, alpha, rho, m, out):
@@ -394,28 +394,36 @@ def tile_sparseadditiveembeddedtopicdecoder_t_kernel(tc, x_bytes, x_scale, wz, b
         def log_root(grp):
             nc.gpsimd.tensor_tensor(out=small("root", grp), in0=live["sum2", grp][:], in1=root_power[:, 0:LOG_BATCHES[grp][1]], op=ALU.pow)
 
-        def log_rest(grp):
-            nc.vector.tensor_scalar(out=small("rest", grp), in0=live["root", grp][:], scalar1=float(V) ** (-1.0 / ROOT),
-                                    scalar2=-1.0, op0=ALU.mult, op1=ALU.add)
-            live["series", grp] = live["rest", grp]
+        def log_start(grp):
+            root = live["root", grp][:]
+            c0 = float(V) ** (-1.0 / ROOT)
+            nc.scalar.activation(out=small("rest", grp), in_=root, func=ACT.Identity, scale=c0, bias=-1.0)
+            nc.scalar.activation(out=small("series0", grp), in_=root, func=ACT.Identity, scale=-c0 / 4, bias=1.0 / 3 + 1.0 / 4)
+            nc.scalar.activation(out=small("lead", grp), in_=root, func=ACT.Identity, scale=-ROOT * c0, bias=float(ROOT))
 
-        def log_term(grp, c):
-            prev = live["series", grp]
-            nxt = work.tile([P, LOG_BATCHES[grp][1]], F32, name="series", tag="series", bufs=2)
-            nc.vector.scalar_tensor_tensor(out=nxt[:], in0=prev[:], scalar=c, in1=live["rest", grp][:], op0=ALU.add, op1=ALU.mult)
-            live["series", grp] = nxt
+        def log_term(grp, src, dst, c):
+            nxt = small(dst, grp)
+            for a in range(LOG_BATCHES[grp][1]):
+                nc.scalar.activation(out=nxt[:, a:a + 1], in_=live[src, grp][:, a:a + 1], func=ACT.Identity,
+                                     scale=live["rest", grp][:, a:a + 1], bias=c)
 
         def log_shift(grp):
-            nc.vector.scalar_tensor_tensor(out=small("shift", grp), in0=live["series", grp][:], scalar=-ROOT / 5.0,
-                                           in1=live["low2", grp][:], op0=ALU.mult, op1=ALU.add)
+            shift = small("shift", grp)
+            for a in range(LOG_BATCHES[grp][1]):
+                nc.scalar.activation(out=shift[:, a:a + 1], in_=live["series2", grp][:, a:a + 1], func=ACT.Identity,
+                                     scale=live["lead", grp][:, a:a + 1], bias=live["low2", grp][:, a:a + 1])
 
-        log_chain = [log_rest, lambda q: log_term(q, -5.0 / 4), lambda q: log_term(q, 5.0 / 3),
-                     lambda q: log_term(q, -5.0 / 2), lambda q: log_term(q, 5.0), log_shift]
+        log_chain = [log_start, lambda q: log_term(q, "series0", "series1", -0.5),
+                     lambda q: log_term(q, "series1", "series2", 1.0), log_shift]
+
+        def log_root_if_last(i):
+            b, a = batch_of[i]
+            if a == LOG_BATCHES[b][1] - 1:
+                log_root(b)
 
         def after_exp2(i):
             b, a = batch_of[i]
             if a == LOG_BATCHES[b][1] - 1:
-                log_root(b)
                 chain_todo.extend((b, link) for link in range(len(log_chain)))
 
         def log_slot():
@@ -425,22 +433,24 @@ def tile_sparseadditiveembeddedtopicdecoder_t_kernel(tc, x_bytes, x_scale, wz, b
                 if link == len(log_chain) - 1:
                     finish_todo.extend(range(LOG_BATCHES[b][0], LOG_BATCHES[b][0] + LOG_BATCHES[b][1]))
 
-        def finish_slot(*engines):
+        def finish_slot(engine, cols=slice(0, V)):
             if finish_todo:
-                finish(finish_todo.pop(0), engines)
+                finish(finish_todo[0], engine, cols)
+                if cols.stop == V:
+                    store(finish_todo.pop(0))
 
-        def finish(i, engines):
+        def finish(i, engine, cols):
             grp, a = batch_of[i]
-            neg = live["neg2", i]
             shift = live["shift", grp][:, a:a + 1]
-            width = V // len(engines)
-            for n, engine in enumerate(engines):
-                part = neg[:, n * width:(n + 1) * width]
-                if engine == "scalar":
-                    nc.scalar.activation(out=part, in_=part, func=ACT.Identity, scale=-1.0, bias=shift)
-                else:
-                    queue = nc.vector if engine == "vector" else nc.gpsimd
-                    queue.tensor_scalar(out=part, in0=part, scalar1=-1.0, scalar2=shift, op0=ALU.mult, op1=ALU.add)
+            part = live["neg2", i][:, cols]
+            if engine == "scalar":
+                nc.scalar.activation(out=part, in_=part, func=ACT.Identity, scale=-1.0, bias=shift)
+            else:
+                queue = nc.vector if engine == "vector" else nc.gpsimd
+                queue.tensor_scalar(out=part, in0=part, scalar1=-1.0, scalar2=shift, op0=ALU.mult, op1=ALU.add)
+
+        def store(i):
+            neg = live["neg2", i]
             grp, a = divmod(i, BATCH_TILES)
             rows = out[grp * BATCH_TILES * P:(grp + 1) * BATCH_TILES * P, :].rearrange("(p a) v -> p a v", a=BATCH_TILES)
             nc.sync.dma_start(out=rows[:, a, :], in_=neg[:])
@@ -468,49 +478,45 @@ def tile_sparseadditiveembeddedtopicdecoder_t_kernel(tc, x_bytes, x_scale, wz, b
                 stage(q)
 
         for step in range(STEPS):
-            drain = step >= TILES
-            tail = step >= TAIL
             if step % BATCH_TILES == 0 and step // BATCH_TILES + 2 < BATCHES:
                 load_x(step // BATCH_TILES + 2)
             on_tile(step, AT_WORDS + 1, lambda i: words_out(i, 1, 2 if step in V_FULL else 1 if step in V_HALF else 0))
+            log_slot()
             for j in tensor_setup.get(step - 1, ()):
                 if j not in ETA_ON_V:
                     eta_out(j, nc.scalar.copy)
             on_tile(step, AT_MAX2, lambda i: max2_turn(i, 0))
             on_tile(step, AT_EXP2, exp2)
+            log_slot()
             on_tile(step, AT_TURN_X, turn_x)
             on_tile(step, 0, scale_x)
-            log_slot()
             if step in vector_setup:
                 vector_setup[step]()
             on_group(step, AT_QUANT_X, quant_x)
             on_group(step, AT_QUANT_C, quant_c)
             root_step = step in root_steps
-            if root_step and not tail:
-                finish_slot("vector", "scalar") if not drain else finish_slot("vector")
+            split = V // 2 if root_step and step < AT_EXP2 + SMALL_FROM else 0
+            if step in CATCH_UP:
+                finish_slot("vector")
+            if split:
+                finish_slot("vector", slice(0, split))
             log_slot()
             on_tile(step, AT_CENTRE, invert)
             on_tile(step, AT_CENTRE, centre)
-            if not root_step and not tail:
-                finish_slot("gpsimd")
-            on_tile(step, AT_EXP2, after_exp2)
+            on_tile(step, AT_EXP2, log_root_if_last)
+            if step <= G_LAST:
+                finish_slot("gpsimd", slice(split, V))
             for j in tensor_setup.get(step - 1, ()):
                 if j in ETA_ON_V:
                     eta_out(j, nc.vector.tensor_copy)
             on_tile(step, AT_MAX2, lambda i: max2(i, 0))
-            if tail:
-                log_slot()
             on_tile(step, AT_LOGITS, logits_mm)
             on_tile(step, AT_MAX1, max1)
             on_tile(step, AT_LOGITS, logits_out)
+            log_slot()
             on_tile(step, AT_MAX1, max1_reduce)
             on_tile(step, AT_MAX2, lambda i: max2_turn(i, 1))
             on_tile(step, AT_MAX2, lambda i: max2(i, 1))
-            if tail:
-                log_slot()
-                finish_slot("vector")
-            if step in S_FINISHES:
-                finish_slot("scalar")
             on_tile(step, AT_MAX1, exp1)
             on_tile(step, AT_GAIN, gain)
             on_tile(step, AT_WORDS, lambda i: words_mm(i, 0))
@@ -520,6 +526,7 @@ def tile_sparseadditiveembeddedtopicdecoder_t_kernel(tc, x_bytes, x_scale, wz, b
                 eta_mm(j)
             if step in scalar_setup:
                 scalar_setup[step]()
+            on_tile(step, AT_EXP2, after_exp2)
         while chain_todo or finish_todo:
             log_slot()
             finish_slot("vector")

@@ -9,7 +9,6 @@ FLOPS = 2 * N * V * K + 2 * K * E * V + 2 * N * K * V
 
 F32 = mybir.dt.float32
 BF16 = mybir.dt.bfloat16
-I32 = mybir.dt.int32
 U32 = mybir.dt.uint32
 U8 = mybir.dt.uint8
 FP8 = mybir.dt.float8_e4m3fn
@@ -19,40 +18,29 @@ ACT = mybir.ActivationFunctionType
 
 P = 128
 PACK = 4
-GROUP_TILES = 2
-GROUP = GROUP_TILES * P
+BANK = 512
 TILES = N // P
-GROUPS = N // GROUP
 WORD_SLICES = V // P
-BATCH_TILES = 4
-BATCHES = TILES // BATCH_TILES
-PER_BANK = 512 // GROUP
+LOAD_TILES = 4
+PAIR = 2
+PAIR_TOKENS = PAIR * P
 
 AT_TURN_X = 1
-AT_QUANT_X = GROUP_TILES + 3
-LEAD = 4
-AT_LOGITS = AT_QUANT_X + 1 + LEAD
-AT_MAX1 = AT_LOGITS + GROUP_TILES
-AT_CENTRE = AT_MAX1 + 1
-AT_GAIN = AT_CENTRE + 1
-AT_QUANT_C = AT_GAIN + GROUP_TILES
-AT_WORDS = AT_QUANT_C
-AT_MAX2 = AT_WORDS + GROUP_TILES
-AT_EXP2 = AT_MAX2 + 1
-SMALL_FROM = 20
-DIAG_TILES = 20
-LOG_BATCHES = [(f, 4) for f in range(0, SMALL_FROM, 4)] + [(f, 2) for f in range(SMALL_FROM, TILES, 2)]
-STEPS = TILES + AT_EXP2 + 1
+AT_QUANT_X = 5
+AT_LOGITS = 8
+AT_SOFTMAX = AT_LOGITS + PAIR
+AT_INVERT = AT_SOFTMAX + 1
+AT_GAIN = AT_INVERT + 1
+AT_WORDS = AT_GAIN + PAIR
+AT_ROW_MAX = AT_WORDS + PAIR
+AT_ROW_SUM = AT_ROW_MAX + 1
+STEPS = TILES + AT_ROW_SUM + 1
+
+DRAIN = TILES + 2
+
+SMALL_BATCHES_FROM = 20
+LOG_BATCHES = [(f, 4) for f in range(0, SMALL_BATCHES_FROM, 4)] + [(f, 2) for f in range(SMALL_BATCHES_FROM, TILES, 2)]
 ROOT = 1024
-ETA_STEPS = {8: (0, 1), 9: (2, 3), 10: (4,), 11: (5,), 12: (6,), 13: (7,)}
-PLAIN_L = 0
-PLAIN_T = 0
-PLAIN_C = 1
-V_HALF = (34, 35, 36, 37, 38, 39, 40, 41)
-V_FULL = (46, 47, 48)
-ETA_ON_V = (1, 3)
-CATCH_UP = (42, 43)
-G_LAST = 48
 
 
 def tile_sparseadditiveembeddedtopicdecoder_t_kernel(tc, x_bytes, x_scale, wz, bz, g, alpha, rho, m, out):
@@ -65,12 +53,9 @@ def tile_sparseadditiveembeddedtopicdecoder_t_kernel(tc, x_bytes, x_scale, wz, b
 
         live = {}
         batch_of = {first + a: (b, a) for b, (first, count) in enumerate(LOG_BATCHES) for a in range(count)}
-        root_steps = [AT_EXP2 + first + count - 1 for first, count in LOG_BATCHES]
-        chain_todo = []
-        finish_todo = []
 
-        def bank(tag):
-            return psum.tile([P, 512], F32, name=tag, tag=tag)
+        def bank(role):
+            return psum.tile([P, BANK], F32, name=role, tag=role)
 
         def wide_tile(shape, dtype):
             return work.tile(shape, dtype, name="wide", tag="wide", bufs=11, align_bytes=64)
@@ -84,47 +69,35 @@ def tile_sparseadditiveembeddedtopicdecoder_t_kernel(tc, x_bytes, x_scale, wz, b
                 rhs=rhs_codes.bitcast(FP8X4), rhs_scale=rhs_scales, start=start, stop=stop,
             )
 
-        def turn(dst, src, plain):
-            if plain:
-                nc.tensor.matmul(dst, lhsT=src, rhs=ident[:], start=True, stop=True)
-            else:
-                nc.tensor.transpose(dst, src, ident[:])
+        def load_x(q):
+            xb = work.tile([P, LOAD_TILES * V], U8, name="xb", tag="xb", bufs=3)
+            rows = x_bytes[q * LOAD_TILES * P:(q + 1) * LOAD_TILES * P, :]
+            nc.sync.dma_start(out=xb[:], in_=rows.rearrange("(n a) v -> n (a v)", a=LOAD_TILES))
+            live["xb", q] = xb
 
-        def tile_at(step, offset):
-            i = step - offset
-            return i if 0 <= i < TILES else None
+        def load_wz(h):
+            raw = keep.tile([P, PACK, K], BF16, name="wz_raw%d" % h)
+            nc.sync.dma_start(out=raw[:], in_=wz[h * 512:(h + 1) * 512, :].rearrange("(p t) c -> p t c", t=PACK))
+            return raw
 
-        def group_at(step, offset, size):
-            q, r = divmod(step - offset, size)
-            return q if r == 0 and 0 <= q < TILES // size else None
-
-        def load_x(grp):
-            xb = work.tile([P, BATCH_TILES * V], U8, name="xb", tag="xb", bufs=3)
-            rows = x_bytes[grp * BATCH_TILES * P:(grp + 1) * BATCH_TILES * P, :]
-            nc.sync.dma_start(out=xb[:], in_=rows.rearrange("(p a) v -> p (a v)", a=BATCH_TILES))
-            live["xb", grp] = xb
+        def load_rho(half):
+            raw = keep.tile([P, PACK, 512], BF16, name="rho_raw%d" % half)
+            nc.sync.dma_start(out=raw[:], in_=rho.rearrange("(p t) v -> p t v", t=PACK)[:, :, half * 512:(half + 1) * 512])
+            return raw
 
         scale_cols = keep.tile([P, 2, PACK], F32)
         nc.sync.dma_start(out=scale_cols[:], in_=x_scale.rearrange("o (h p t) -> p (o h) t", p=P, t=PACK))
-        wz_raw = []
-        for h in range(2):
-            if h == 1:
-                load_x(0)
-            raw = keep.tile([P, PACK, K], BF16, name="wz_raw%d" % h)
-            nc.sync.dma_start(out=raw[:], in_=wz[h * 512:(h + 1) * 512, :].rearrange("(p j) c -> p j c", j=PACK))
-            wz_raw.append(raw)
+        wz_raw = [load_wz(0)]
+        load_x(0)
+        wz_raw.append(load_wz(1))
         bz_raw = keep.tile([P, PACK], BF16)
         nc.sync.dma_start(out=bz_raw[:], in_=bz.rearrange("(p t) -> p t", t=PACK))
         g_raw = keep.tile([P, PACK], BF16)
         nc.sync.dma_start(out=g_raw[:], in_=g.rearrange("(p t) -> p t", t=PACK))
         load_x(1)
         alpha_raw = keep.tile([P, PACK, E], BF16)
-        nc.sync.dma_start(out=alpha_raw[:], in_=alpha.rearrange("(p t) e -> p t e", t=PACK))
-        rho_raw = []
-        for h in range(2):
-            raw = keep.tile([P, PACK, 512], BF16, name="rho_raw%d" % h)
-            nc.sync.dma_start(out=raw[:], in_=rho.rearrange("(p j) v -> p j v", j=PACK)[:, :, h * 512:(h + 1) * 512])
-            rho_raw.append(raw)
+        nc.sync.dma_start(out=alpha_raw[:], in_=alpha.rearrange("(r t) e -> r t e", t=PACK))
+        rho_raw = [load_rho(0), load_rho(1)]
 
         ident = keep.tile([P, P], F32)
         make_identity(nc, ident[:])
@@ -134,11 +107,11 @@ def tile_sparseadditiveembeddedtopicdecoder_t_kernel(tc, x_bytes, x_scale, wz, b
 
         x_scales = keep.tile([P, V], F32)
         for u in range(2):
-            spread = bank("word_bank%d" % u)
-            for q in range(4):
-                h, e = divmod(q, 2)
-                col = scale_cols[:, h, 2 * u + e:2 * u + e + 1].to_broadcast([P, P])
-                nc.tensor.transpose(spread[:, q * P:(q + 1) * P], col, ident[:])
+            spread = bank("row_bank%d" % u)
+            for h in range(2):
+                for e in range(2):
+                    col = scale_cols[:, h, 2 * u + e:2 * u + e + 1].to_broadcast([P, P])
+                    nc.tensor.transpose(spread[:, (2 * h + e) * P:(2 * h + e + 1) * P], col, ident[:])
             nc.scalar.activation(
                 out=x_scales[:, u * 512:(u + 1) * 512].rearrange("n (h p e) -> n h p e", h=2, e=2),
                 in_=spread[:].rearrange("n (h e p) -> n h p e", h=2, e=2), func=ACT.Copy,
@@ -152,60 +125,67 @@ def tile_sparseadditiveembeddedtopicdecoder_t_kernel(tc, x_bytes, x_scale, wz, b
         rho_scales = keep.tile([P, V], U8, align_bytes=64)
         eta_codes = keep.tile([P, V], U32, align_bytes=64)
         eta_scales = keep.tile([P, V], U8, align_bytes=64)
-        bz_cols = keep.tile([P, PACK], F32)
+        neg_bz_cols = keep.tile([P, PACK], F32)
         gain_cols = keep.tile([P, PACK], F32)
+        gain_rows = keep.tile([P, K], F32)
         m_rows32 = keep.tile([P, P], F32)
         m_cols = keep.tile([P, WORD_SLICES], F32)
         exp_sink = keep.tile([P, V], BF16)
-        root_power = keep.tile([P, BATCH_TILES], F32)
+        root_power = keep.tile([P, LOG_BATCHES[0][1]], F32)
         nc.gpsimd.memset(root_power[:], 1.0 / ROOT)
 
         def group_wz(h, part, copy):
             if part == 0:
                 live["wz", h] = wide_tile([P, K * PACK], BF16)
-            slots = slice(2 * part, 2 * part + 2)
-            copy(out=live["wz", h][:].rearrange("p (t q j) -> p t q j", t=PACK, j=PACK)[:, slots],
-                           in_=wz_raw[h][:].rearrange("p j (q t) -> p t q j", t=PACK)[:, slots])
+            slices = slice(2 * part, 2 * part + 2)
+            copy(out=live["wz", h][:].rearrange("p (s r t) -> p s r t", s=PACK, t=PACK)[:, slices],
+                 in_=wz_raw[h][:].rearrange("p t (r s) -> p s r t", s=PACK)[:, slices])
 
         def quant_wz(h):
             quantise(wz_codes[:, h, :], wz_scales[:, h, :], live["wz", h][:])
 
         def cast_vectors():
-            nc.vector.tensor_scalar(out=bz_cols[:], in0=bz_raw[:], scalar1=-1.0, scalar2=None, op0=ALU.mult)
+            nc.vector.tensor_scalar(out=neg_bz_cols[:], in0=bz_raw[:], scalar1=-1.0, scalar2=None, op0=ALU.mult)
             nc.vector.tensor_scalar(out=gain_cols[:], in0=g_raw[:], scalar1=float(K), scalar2=None, op0=ALU.mult)
+
+        def spread_gain():
+            nc.scalar.copy(out=gain_rows[:].rearrange("p (n t) -> p n t", t=PACK),
+                           in_=gain_cols[:].unsqueeze(1).to_broadcast([P, P, PACK]))
 
         def turn_alpha():
             grouped = wide_tile([P, K * PACK], BF16)
-            pairs = grouped[:].bitcast(F32).rearrange("p (t q u) -> p t q u", t=PACK, u=2)
-            for half, tag in enumerate(("logit_bank", "centre_bank")):
-                turned = bank(tag)
-                for tt in range(2):
-                    words = alpha_raw[:, 2 * half + tt, :].bitcast(F32)
+            pairs = grouped[:].bitcast(F32).rearrange("p (s r u) -> p s r u", s=PACK, u=2)
+            for half, role in enumerate(("logit_bank", "gain_bank")):
+                turned = bank(role)
+                for s in range(2):
+                    words = alpha_raw[:, 2 * half + s, :].bitcast(F32)
                     for u in range(2):
-                        q = 2 * tt + u
-                        nc.tensor.transpose(turned[:, q * P:(q + 1) * P], words[:, u:2 * P:2], ident[:])
+                        nc.tensor.transpose(turned[:, (2 * s + u) * P:(2 * s + u + 1) * P], words[:, u:2 * P:2], ident[:])
                 nc.scalar.copy(out=pairs[:, 2 * half:2 * half + 2, :, :],
-                               in_=turned[:].rearrange("p (t u q) -> p t q u", t=2, u=2))
+                               in_=turned[:].rearrange("p (s u r) -> p s r u", s=2, u=2))
             live["alpha"] = grouped
 
-        def group_rho(h, part):
-            if part == 0:
-                live["rho", h] = wide_tile([P, 512 * PACK], BF16)
-            nc.scalar.copy(out=live["rho", h][:, part * 1024:(part + 1) * 1024].rearrange("p (c i j) -> p c j i", i=4, j=PACK),
-                           in_=rho_raw[h][:, :, part * 256:(part + 1) * 256].rearrange("p j (c i) -> p c j i", i=4))
+        def quant_alpha():
+            quantise(alpha_codes[:], alpha_scales[:], live["alpha"][:])
 
-        def quant_rho(h):
-            cols = slice(h * 512, (h + 1) * 512)
-            quantise(rho_codes[:, cols], rho_scales[:, cols], live["rho", h][:])
+        def group_rho(half, part, copy):
+            if part == 0:
+                live["rho", half] = wide_tile([P, 512 * PACK], BF16)
+            copy(out=live["rho", half][:, part * 1024:(part + 1) * 1024].rearrange("p (c i t) -> p c t i", i=4, t=PACK),
+                 in_=rho_raw[half][:, :, part * 256:(part + 1) * 256].rearrange("p t (c i) -> p c t i", i=4))
+
+        def quant_rho(half):
+            cols = slice(half * 512, (half + 1) * 512)
+            quantise(rho_codes[:, cols], rho_scales[:, cols], live["rho", half][:])
 
         def turn_m():
             nc.scalar.copy(out=m_rows32[:], in_=m_rows[:])
-            turned = bank("centre_bank")
+            turned = bank("gain_bank")
             nc.tensor.transpose(turned[:, 0:P], m_rows32[:], ident[:])
             nc.scalar.copy(out=m_cols[:], in_=turned[:, 0:WORD_SLICES])
 
         def eta_mm(j):
-            acc = bank(("logit_bank", "centre_bank")[j % 2] if j in (2, 3) else "word_bank%d" % (j % 2))
+            acc = bank("row_bank%d" % (j % 2))
             cols = slice(j * P, (j + 1) * P)
             for t in range(PACK):
                 topics = slice(t * P, (t + 1) * P)
@@ -214,319 +194,322 @@ def tile_sparseadditiveembeddedtopicdecoder_t_kernel(tc, x_bytes, x_scale, wz, b
             live["eta_acc", j] = acc
 
         def eta_out(j, copy):
-            h, r = divmod(j, 4)
-            if ("eta", h) not in live:
-                live["eta", h] = wide_tile([P, 512 * PACK], BF16)
-            acc = live["eta_acc", j]
-            copy(out=live["eta", h][:, r * 512:(r + 1) * 512].rearrange("p (w t) -> p w t", t=PACK),
-                           in_=acc[:].rearrange("p (t w) -> p w t", t=PACK))
+            half, r = divmod(j, 4)
+            if r == 0:
+                live["eta", half] = wide_tile([P, 512 * PACK], BF16)
+            copy(out=live["eta", half][:, r * 512:(r + 1) * 512].rearrange("p (w t) -> p w t", t=PACK),
+                 in_=live["eta_acc", j][:].rearrange("p (t w) -> p w t", t=PACK))
 
-        def quant_eta(h):
-            cols = slice(h * 512, (h + 1) * 512)
-            quantise(eta_codes[:, cols], eta_scales[:, cols], live["eta", h][:])
+        def quant_eta(half):
+            cols = slice(half * 512, (half + 1) * 512)
+            quantise(eta_codes[:, cols], eta_scales[:, cols], live["eta", half][:])
 
         def scale_x(i):
-            grp, a = divmod(i, BATCH_TILES)
+            q, a = divmod(i, LOAD_TILES)
             xs = work.tile([P, V], BF16, name="xs", tag="xs", bufs=4)
-            codes = live["xb", grp][:, a * V:(a + 1) * V].bitcast(FP8)
+            codes = live["xb", q][:, a * V:(a + 1) * V].bitcast(FP8)
             nc.vector.tensor_tensor(
-                out=xs[:].rearrange("n (u q e) -> n u q e", u=2, e=2),
-                in0=codes.rearrange("n (q u e) -> n u q e", u=2, e=2),
-                in1=x_scales[:].rearrange("n (u q e) -> n u q e", u=2, e=2), op=ALU.mult,
+                out=xs[:].rearrange("n (u c e) -> n u c e", u=2, e=2),
+                in0=codes.rearrange("n (c u e) -> n u c e", u=2, e=2),
+                in1=x_scales[:].rearrange("n (u c e) -> n u c e", u=2, e=2), op=ALU.mult,
             )
             live["xs", i] = xs
 
         def turn_x(i):
-            grp, a = divmod(i, GROUP_TILES)
+            pair, a = divmod(i, PAIR)
             if a == 0:
-                live["xw", grp] = work.tile([P, 2, GROUP * PACK], BF16, name="xw", tag="xw", bufs=3, align_bytes=64)
+                live["xw", pair] = work.tile([P, 2, PAIR_TOKENS * PACK], BF16, name="xw", tag="xw", bufs=3, align_bytes=64)
             words = live["xs", i][:].bitcast(F32)
             turned = bank("x_bank")
-            for q in range(4):
-                nc.tensor.transpose(turned[:, q * P:(q + 1) * P], words[:, q * P:(q + 1) * P], ident[:])
-            pairs = live["xw", grp][:].bitcast(F32).rearrange("p h (n u) -> p h n u", u=2)
-            nc.scalar.copy(out=pairs[:, :, a * P:(a + 1) * P, :],
+            for c in range(4):
+                nc.tensor.transpose(turned[:, c * P:(c + 1) * P], words[:, c * P:(c + 1) * P], ident[:])
+            tokens = live["xw", pair][:].bitcast(F32).rearrange("p h (n u) -> p h n u", u=2)
+            nc.scalar.copy(out=tokens[:, :, a * P:(a + 1) * P, :],
                            in_=turned[:].rearrange("p (u h n) -> p h n u", u=2, h=2))
 
-        def quant_x(grp):
-            codes = work.tile([P, 2, GROUP], U32, name="x_codes", tag="x_codes", bufs=2 + LEAD // 2, align_bytes=64)
-            scales = work.tile([P, 2, GROUP], U8, name="x_mx_scales", tag="x_mx_scales", bufs=2 + LEAD // 2, align_bytes=64)
+        def quant_x(pair):
+            codes = work.tile([P, 2, PAIR_TOKENS], U32, name="x_codes", tag="x_codes", bufs=4, align_bytes=64)
+            scales = work.tile([P, 2, PAIR_TOKENS], U8, name="x_mx_scales", tag="x_mx_scales", bufs=4, align_bytes=64)
             quantise(codes[:].rearrange("p h n -> p (h n)"), scales[:].rearrange("p h n -> p (h n)"),
-                     live["xw", grp][:].rearrange("p h n -> p (h n)"))
-            live["xq", grp] = (codes, scales)
+                     live["xw", pair][:].rearrange("p h n -> p (h n)"))
+            live["xq", pair] = (codes, scales)
 
         def logits_mm(i):
-            grp, a = divmod(i, GROUP_TILES)
+            pair, a = divmod(i, PAIR)
             acc = bank("mx_bank2")
-            codes, scales = live["xq", grp]
-            for r in range(PER_BANK):
-                t = a * PER_BANK + r
-                topics = slice(t * P, (t + 1) * P)
+            codes, scales = live["xq", pair]
+            for r in range(2):
+                topics = slice((2 * a + r) * P, (2 * a + r + 1) * P)
                 for h in range(2):
-                    mx_pass(acc[:, r * GROUP:(r + 1) * GROUP], wz_codes[:, h, topics], wz_scales[:, h, topics],
+                    mx_pass(acc[:, r * PAIR_TOKENS:(r + 1) * PAIR_TOKENS], wz_codes[:, h, topics], wz_scales[:, h, topics],
                             codes[:, h, :], scales[:, h, :], h == 0, h == 1)
             live["logit_acc"] = acc
 
         def logits_out(i):
-            grp, a = divmod(i, GROUP_TILES)
-            for r in range(PER_BANK):
-                t = a * PER_BANK + r
-                lt = work.tile([P, GROUP], F32, name="lt", tag="lt", bufs=8)
-                nc.scalar.activation(out=lt[:], in_=live["logit_acc"][:, r * GROUP:(r + 1) * GROUP], func=ACT.Identity,
-                                     scale=-1.0, bias=bz_cols[:, t:t + 1])
-                live["lt", grp, t] = lt
+            pair, a = divmod(i, PAIR)
+            for r in range(2):
+                t = 2 * a + r
+                neg_logits = work.tile([P, PAIR_TOKENS], F32, name="neg_logits", tag="neg_logits", bufs=8)
+                nc.scalar.activation(out=neg_logits[:], in_=live["logit_acc"][:, r * PAIR_TOKENS:(r + 1) * PAIR_TOKENS],
+                                     func=ACT.Identity, scale=-1.0, bias=neg_bz_cols[:, t:t + 1])
+                live["neg_logits", pair, t] = neg_logits
 
-        def max1(i):
-            grp, a = divmod(i, GROUP_TILES)
+        def turn_logits(i):
+            pair, a = divmod(i, PAIR)
             turned = bank("logit_bank")
             for t in range(PACK):
-                turn(turned[:, t * P:(t + 1) * P], live["lt", grp, t][:, a * P:(a + 1) * P], t < PLAIN_L)
-            live["turned1"] = turned
+                nc.tensor.transpose(turned[:, t * P:(t + 1) * P], live["neg_logits", pair, t][:, a * P:(a + 1) * P], ident[:])
+            live["logit_rows", i] = turned
 
-        def max1_reduce(i):
-            turned = live["turned1"]
-            low = work.tile([P, 1], F32, name="neg_max1", tag="neg_max1", bufs=3)
-            nc.vector.tensor_reduce(out=low[:], in_=turned[:], axis=mybir.AxisListType.X, op=ALU.min)
-            live["neg1", i] = (turned, low)
+        def logit_max(i):
+            neg_max = work.tile([P, 1], F32, name="neg_logit_max", tag="neg_logit_max", bufs=3)
+            nc.vector.tensor_reduce(out=neg_max[:], in_=live["logit_rows", i][:], axis=mybir.AxisListType.X, op=ALU.min)
+            live["neg_logit_max", i] = neg_max
 
-        def exp1(i):
-            neg, low = live["neg1", i]
-            e1 = work.tile([P, K], F32, name="e1", tag="e1", bufs=4)
-            total = work.tile([P, 1], F32, name="sum1", tag="sum1", bufs=3)
-            nc.scalar.activation(out=e1[:], in_=neg[:], func=ACT.Exp, scale=-1.0, bias=low[:], accum_out=total[:])
-            live["e1", i] = (e1, total)
+        def logit_exp(i):
+            powers = work.tile([P, K], F32, name="powers", tag="powers", bufs=4)
+            total = work.tile([P, 1], F32, name="power_sum", tag="power_sum", bufs=3)
+            nc.scalar.activation(out=powers[:], in_=live["logit_rows", i][:], func=ACT.Exp, scale=-1.0,
+                                 bias=live["neg_logit_max", i][:], accum_out=total[:])
+            live["powers", i] = powers
+            live["power_sum", i] = total
+
+        def by_diagonal(i):
+            return i + AT_GAIN < DRAIN
 
         def invert(i):
-            inv = work.tile([P, 1], F32, name="inv1", tag="inv1", bufs=3)
-            nc.vector.reciprocal(out=inv[:], in_=live["e1", i][1][:])
-            live["inv", i] = inv
-
-        def centre(i):
-            if i < DIAG_TILES:
-                d = work.tile([P, P], F32, name="inv_diag", tag="inv_diag", bufs=3)
-                nc.gpsimd.tensor_scalar(out=d[:], in0=ident[:], scalar1=live["inv", i][:], scalar2=1.0, op0=ALU.mult, op1=ALU.mult)
+            inv = work.tile([P, 1], F32, name="inv_sum", tag="inv_sum", bufs=3)
+            nc.vector.reciprocal(out=inv[:], in_=live["power_sum", i][:])
+            if by_diagonal(i):
+                scaled = work.tile([P, P], F32, name="inv_diag", tag="inv_diag", bufs=3)
+                source = ident
             else:
-                d = work.tile([P, K], F32, name="centred", tag="centred", bufs=3)
-                nc.gpsimd.tensor_scalar(out=d[:], in0=live["e1", i][0][:], scalar1=live["inv", i][:], scalar2=1.0,
-                                        op0=ALU.mult, op1=ALU.mult)
-            live["d", i] = d
+                scaled = work.tile([P, K], F32, name="theta", tag="theta", bufs=3)
+                source = live["powers", i]
+            nc.gpsimd.tensor_scalar(out=scaled[:], in0=source[:], scalar1=inv[:], scalar2=1.0, op0=ALU.mult, op1=ALU.mult)
+            live["scaled", i] = scaled
 
         def gain(i):
-            grp, a = divmod(i, GROUP_TILES)
+            pair, a = divmod(i, PAIR)
             if a == 0:
-                live["cb", grp] = work.tile([P, GROUP * PACK], BF16, name="cb", tag="cb", bufs=2, align_bytes=64)
-            turned = bank("centre_bank")
-            for t in range(PACK):
-                if i < DIAG_TILES:
-                    nc.tensor.matmul(turned[:, t * P:(t + 1) * P], lhsT=live["e1", i][0][:, t * P:(t + 1) * P], rhs=live["d", i][:],
+                live["c", pair] = work.tile([P, PAIR_TOKENS * PACK], BF16, name="c", tag="c", bufs=2, align_bytes=64)
+            c_tile = live["c", pair][:, a * K:(a + 1) * K]
+            turned = bank("gain_bank")
+            if by_diagonal(i):
+                for t in range(PACK):
+                    nc.tensor.matmul(turned[:, t:K:PACK], lhsT=live["powers", i][:, t * P:(t + 1) * P], rhs=live["scaled", i][:],
                                      start=True, stop=True)
-                else:
-                    turn(turned[:, t * P:(t + 1) * P], live["d", i][:, t * P:(t + 1) * P], t >= PACK - PLAIN_C)
-            nc.vector.scalar_tensor_tensor(
-                out=live["cb", grp][:, a * 512:(a + 1) * 512].rearrange("p (n t) -> p n t", t=PACK),
-                in0=turned[:].rearrange("p (t n) -> p n t", t=PACK), scalar=-1.0 / K,
-                in1=gain_cols[:].unsqueeze(1).to_broadcast([P, P, PACK]), op0=ALU.add, op1=ALU.mult,
-            )
+                nc.vector.scalar_tensor_tensor(out=c_tile, in0=turned[:], scalar=-1.0 / K, in1=gain_rows[:],
+                                               op0=ALU.add, op1=ALU.mult)
+            else:
+                for t in range(PACK):
+                    nc.tensor.transpose(turned[:, t * P:(t + 1) * P], live["scaled", i][:, t * P:(t + 1) * P], ident[:])
+                nc.vector.scalar_tensor_tensor(
+                    out=c_tile.rearrange("p (n t) -> p n t", t=PACK), in0=turned[:].rearrange("p (t n) -> p n t", t=PACK),
+                    scalar=-1.0 / K, in1=gain_cols[:].unsqueeze(1).to_broadcast([P, P, PACK]), op0=ALU.add, op1=ALU.mult,
+                )
 
-        def quant_c(grp):
-            codes = work.tile([P, GROUP], U32, name="c_codes", tag="c_codes", bufs=2, align_bytes=64)
-            scales = work.tile([P, GROUP], U8, name="c_mx_scales", tag="c_mx_scales", bufs=2, align_bytes=64)
-            quantise(codes[:], scales[:], live["cb", grp][:])
-            live["cq", grp] = (codes, scales)
+        def quant_c(pair):
+            codes = work.tile([P, PAIR_TOKENS], U32, name="c_codes", tag="c_codes", bufs=2, align_bytes=64)
+            scales = work.tile([P, PAIR_TOKENS], U8, name="c_mx_scales", tag="c_mx_scales", bufs=2, align_bytes=64)
+            quantise(codes[:], scales[:], live["c", pair][:])
+            live["cq", pair] = (codes, scales)
 
         def words_mm(i, b):
-            grp, a = divmod(i, GROUP_TILES)
+            pair, a = divmod(i, PAIR)
             acc = bank("mx_bank%d" % b)
-            codes, scales = live["cq", grp]
-            for r in range(PER_BANK):
-                j = (2 * a + b) * PER_BANK + r
+            codes, scales = live["cq", pair]
+            for r in range(2):
+                j = 4 * a + 2 * b + r
                 cols = slice(j * P, (j + 1) * P)
-                mx_pass(acc[:, r * GROUP:(r + 1) * GROUP], eta_codes[:, cols], eta_scales[:, cols], codes[:], scales[:], True, True)
+                mx_pass(acc[:, r * PAIR_TOKENS:(r + 1) * PAIR_TOKENS], eta_codes[:, cols], eta_scales[:, cols],
+                        codes[:], scales[:], True, True)
             live["word_acc", b] = acc
 
         def words_out(i, b, on_vector):
-            grp, a = divmod(i, GROUP_TILES)
-            for r in range(PER_BANK):
-                j = (2 * a + b) * PER_BANK + r
-                tt = work.tile([P, GROUP], F32, name="tt", tag="tt", bufs=16)
-                acc = live["word_acc", b][:, r * GROUP:(r + 1) * GROUP]
+            pair, a = divmod(i, PAIR)
+            for r in range(2):
+                j = 4 * a + 2 * b + r
+                t_slice = work.tile([P, PAIR_TOKENS], F32, name="t_slice", tag="t_slice", bufs=16)
+                acc = live["word_acc", b][:, r * PAIR_TOKENS:(r + 1) * PAIR_TOKENS]
                 if r < on_vector:
-                    nc.vector.tensor_scalar(out=tt[:], in0=acc, scalar1=1.0 / math.sqrt(K),
+                    nc.vector.tensor_scalar(out=t_slice[:], in0=acc, scalar1=1.0 / math.sqrt(K),
                                             scalar2=m_cols[:, j:j + 1], op0=ALU.mult, op1=ALU.add)
                 else:
-                    nc.scalar.activation(out=tt[:], in_=acc, func=ACT.Identity,
+                    nc.scalar.activation(out=t_slice[:], in_=acc, func=ACT.Identity,
                                          scale=1.0 / math.sqrt(K), bias=m_cols[:, j:j + 1])
-                live["tt", grp, j] = tt
+                live["t_slice", pair, j] = t_slice
 
-        def max2_turn(i, half):
-            grp, a = divmod(i, GROUP_TILES)
-            turned = bank("word_bank%d" % half)
+        def batch_tile(key, b, bufs):
+            columns = work.tile([P, LOG_BATCHES[b][1]], F32, name=key, tag=key, bufs=bufs)
+            live[key, b] = columns
+            return columns
+
+        def turn_rows(i, half):
+            pair, a = divmod(i, PAIR)
+            turned = bank("row_bank%d" % half)
             for r in range(4):
-                turn(turned[:, r * P:(r + 1) * P], live["tt", grp, 4 * half + r][:, a * P:(a + 1) * P], half == 1 and r < PLAIN_T)
-            live["turned2", half] = turned
+                nc.tensor.transpose(turned[:, r * P:(r + 1) * P], live["t_slice", pair, 4 * half + r][:, a * P:(a + 1) * P], ident[:])
+            live["t_rows", half] = turned
 
-        def max2(i, half):
-            grp, a = batch_of[i]
+        def row_max(i, half):
+            b, a = batch_of[i]
             if half == 0:
-                live["neg2", i] = wide_tile([P, V], F32)
-                live["low_half", i] = work.tile([P, 1], F32, name="low_half", tag="low_half", bufs=2)
+                live["neg_t", i] = wide_tile([P, V], F32)
+                live["half_min", i] = work.tile([P, 1], F32, name="half_min", tag="half_min", bufs=2)
                 if a == 0:
-                    live["low2", grp] = work.tile([P, LOG_BATCHES[grp][1]], F32, name="neg_max2", tag="neg_max2", bufs=4)
-            turned = live["turned2", half]
+                    batch_tile("neg_max", b, 4)
             nc.vector.tensor_scalar(
-                out=live["neg2", i][:, half * 512:(half + 1) * 512], in0=turned[:], scalar1=-1.0,
-                scalar2=None if half == 0 else live["low_half", i][:], op0=ALU.mult, op1=ALU.min,
-                accum_out=live["low_half", i][:] if half == 0 else live["low2", grp][:, a:a + 1],
+                out=live["neg_t", i][:, half * BANK:(half + 1) * BANK], in0=live["t_rows", half][:], scalar1=-1.0,
+                scalar2=None if half == 0 else live["half_min", i][:], op0=ALU.mult, op1=ALU.min,
+                accum_out=live["half_min", i][:] if half == 0 else live["neg_max", b][:, a:a + 1],
             )
 
-        def exp2(i):
-            grp, a = batch_of[i]
+        def row_sum(i):
+            b, a = batch_of[i]
             if a == 0:
-                live["sum2", grp] = work.tile([P, LOG_BATCHES[grp][1]], F32, name="sum2", tag="sum2", bufs=3)
-            nc.scalar.activation(out=exp_sink[:], in_=live["neg2", i][:], func=ACT.Exp, scale=-1.0,
-                                 bias=live["low2", grp][:, a:a + 1], accum_out=live["sum2", grp][:, a:a + 1])
+                batch_tile("row_sums", b, 3)
+            nc.scalar.activation(out=exp_sink[:], in_=live["neg_t", i][:], func=ACT.Exp, scale=-1.0,
+                                 bias=live["neg_max", b][:, a:a + 1], accum_out=live["row_sums", b][:, a:a + 1])
 
-        def small(key, grp):
-            t = work.tile([P, LOG_BATCHES[grp][1]], F32, name=key, tag=key, bufs=3)
-            live[key, grp] = t
-            return t[:]
+        def log_root(b):
+            nc.gpsimd.tensor_tensor(out=batch_tile("root", b, 3)[:], in0=live["row_sums", b][:],
+                                    in1=root_power[:, 0:LOG_BATCHES[b][1]], op=ALU.pow)
 
-        def log_root(grp):
-            nc.gpsimd.tensor_tensor(out=small("root", grp), in0=live["sum2", grp][:], in1=root_power[:, 0:LOG_BATCHES[grp][1]], op=ALU.pow)
+        def log_start(b):
+            root = live["root", b][:]
+            centre = float(V) ** (-1.0 / ROOT)
+            nc.scalar.activation(out=batch_tile("horner0", b, 3)[:], in_=root, func=ACT.Identity,
+                                 scale=-centre / 4 / ROOT ** 2, bias=(1.0 / 3 + 1.0 / 4) / ROOT ** 2)
+            nc.scalar.activation(out=batch_tile("w", b, 3)[:], in_=root, func=ACT.Identity, scale=-ROOT * centre, bias=float(ROOT))
 
-        def log_start(grp):
-            root = live["root", grp][:]
-            c0 = float(V) ** (-1.0 / ROOT)
-            nc.scalar.activation(out=small("rest", grp), in_=root, func=ACT.Identity, scale=c0, bias=-1.0)
-            nc.scalar.activation(out=small("series0", grp), in_=root, func=ACT.Identity, scale=-c0 / 4, bias=1.0 / 3 + 1.0 / 4)
-            nc.scalar.activation(out=small("lead", grp), in_=root, func=ACT.Identity, scale=-ROOT * c0, bias=float(ROOT))
+        def log_step(b, src, dst, bias_of):
+            result = batch_tile(dst, b, 3)
+            for a in range(LOG_BATCHES[b][1]):
+                nc.scalar.activation(out=result[:, a:a + 1], in_=live[src, b][:, a:a + 1], func=ACT.Identity,
+                                     scale=live["w", b][:, a:a + 1], bias=bias_of(a))
 
-        def log_term(grp, src, dst, c):
-            nxt = small(dst, grp)
-            for a in range(LOG_BATCHES[grp][1]):
-                nc.scalar.activation(out=nxt[:, a:a + 1], in_=live[src, grp][:, a:a + 1], func=ACT.Identity,
-                                     scale=live["rest", grp][:, a:a + 1], bias=c)
+        series = [
+            log_start,
+            lambda b: log_step(b, "horner0", "horner1", lambda a: 0.5 / ROOT),
+            lambda b: log_step(b, "horner1", "horner2", lambda a: 1.0),
+            lambda b: log_step(b, "horner2", "shift", lambda a: live["neg_max", b][:, a:a + 1]),
+        ]
+        series_todo = []
+        finish_todo = []
 
-        def log_shift(grp):
-            shift = small("shift", grp)
-            for a in range(LOG_BATCHES[grp][1]):
-                nc.scalar.activation(out=shift[:, a:a + 1], in_=live["series2", grp][:, a:a + 1], func=ACT.Identity,
-                                     scale=live["lead", grp][:, a:a + 1], bias=live["low2", grp][:, a:a + 1])
-
-        log_chain = [log_start, lambda q: log_term(q, "series0", "series1", -0.5),
-                     lambda q: log_term(q, "series1", "series2", 1.0), log_shift]
-
-        def log_root_if_last(i):
+        def closes_batch(i):
             b, a = batch_of[i]
-            if a == LOG_BATCHES[b][1] - 1:
-                log_root(b)
+            return a == LOG_BATCHES[b][1] - 1
 
-        def after_exp2(i):
-            b, a = batch_of[i]
-            if a == LOG_BATCHES[b][1] - 1:
-                chain_todo.extend((b, link) for link in range(len(log_chain)))
+        def take_root(i):
+            if closes_batch(i):
+                log_root(batch_of[i][0])
 
-        def log_slot():
-            if chain_todo:
-                b, link = chain_todo.pop(0)
-                log_chain[link](b)
-                if link == len(log_chain) - 1:
-                    finish_todo.extend(range(LOG_BATCHES[b][0], LOG_BATCHES[b][0] + LOG_BATCHES[b][1]))
+        def queue_series(i):
+            if closes_batch(i):
+                series_todo.extend((batch_of[i][0], link) for link in range(len(series)))
 
-        def finish_slot(engine, cols=slice(0, V)):
+        def series_slot():
+            if series_todo:
+                b, link = series_todo.pop(0)
+                series[link](b)
+                if link == len(series) - 1:
+                    first, count = LOG_BATCHES[b]
+                    finish_todo.extend(range(first, first + count))
+
+        def finish_slot(engine, cols):
             if finish_todo:
-                finish(finish_todo[0], engine, cols)
+                i = finish_todo[0]
+                b, a = batch_of[i]
+                part = live["neg_t", i][:, cols]
+                engine.tensor_scalar(out=part, in0=part, scalar1=-1.0, scalar2=live["shift", b][:, a:a + 1],
+                                     op0=ALU.mult, op1=ALU.add)
                 if cols.stop == V:
-                    store(finish_todo.pop(0))
+                    q, a = divmod(finish_todo.pop(0), LOAD_TILES)
+                    rows = out[q * LOAD_TILES * P:(q + 1) * LOAD_TILES * P, :].rearrange("(n a) v -> n a v", a=LOAD_TILES)
+                    nc.sync.dma_start(out=rows[:, a, :], in_=live["neg_t", i][:])
 
-        def finish(i, engine, cols):
-            grp, a = batch_of[i]
-            shift = live["shift", grp][:, a:a + 1]
-            part = live["neg2", i][:, cols]
-            if engine == "scalar":
-                nc.scalar.activation(out=part, in_=part, func=ACT.Identity, scale=-1.0, bias=shift)
-            else:
-                queue = nc.vector if engine == "vector" else nc.gpsimd
-                queue.tensor_scalar(out=part, in0=part, scalar1=-1.0, scalar2=shift, op0=ALU.mult, op1=ALU.add)
-
-        def store(i):
-            neg = live["neg2", i]
-            grp, a = divmod(i, BATCH_TILES)
-            rows = out[grp * BATCH_TILES * P:(grp + 1) * BATCH_TILES * P, :].rearrange("(p a) v -> p a v", a=BATCH_TILES)
-            nc.sync.dma_start(out=rows[:, a, :], in_=neg[:])
-
-        vector_setup = {
-            1: cast_vectors, 2: lambda: quant_wz(0), 3: lambda: quant_wz(1),
-            4: lambda: quantise(alpha_codes[:], alpha_scales[:], live["alpha"][:]),
-            6: lambda: quant_rho(0), 8: lambda: quant_rho(1), AT_WORDS - 4: lambda: quant_eta(0), AT_WORDS: lambda: quant_eta(1),
+        vector_prep = {
+            1: cast_vectors, 2: lambda: quant_wz(0), 3: lambda: quant_wz(1), 4: quant_alpha,
+            6: lambda: (quant_rho(0), group_rho(1, 1, nc.vector.tensor_copy)), 7: lambda: quant_rho(1),
+            AT_SOFTMAX: lambda: quant_eta(0), AT_WORDS: lambda: quant_eta(1),
         }
-        scalar_setup = {0: lambda: group_wz(1, 0, nc.scalar.copy), 1: lambda: group_wz(1, 1, nc.scalar.copy), 2: turn_alpha,
-                        3: lambda: group_rho(0, 0), 4: lambda: group_rho(0, 1), 5: lambda: group_rho(1, 0),
-                        6: lambda: group_rho(1, 1), 7: turn_m}
-        tensor_setup = ETA_STEPS
-        group_wz(0, 0, nc.vector.tensor_copy)
-        group_wz(0, 1, nc.vector.tensor_copy)
+        scalar_prep = {
+            0: lambda: group_wz(1, 0, nc.scalar.copy), 1: lambda: group_wz(1, 1, nc.scalar.copy), 2: turn_alpha,
+            3: lambda: group_rho(0, 0, nc.scalar.copy), 4: lambda: group_rho(0, 1, nc.scalar.copy),
+            5: lambda: group_rho(1, 0, nc.scalar.copy), 6: turn_m, 7: spread_gain,
+        }
+        eta_steps = {7: (0, 1), 8: (2, 3), 9: (4, 5), 10: (6,), 11: (7,)}
+        eta_on_vector = (3, 5)
+        root_steps = [AT_ROW_SUM + first + count - 1 for first, count in LOG_BATCHES if count == 4]
+
+        def slices_on_vector(step):
+            if step >= TILES + AT_GAIN:
+                return 2
+            return 1 if DRAIN <= step < TILES + AT_LOGITS or step - 1 in root_steps else 0
 
         def on_tile(step, offset, stage):
-            i = tile_at(step, offset)
-            if i is not None:
-                stage(i)
+            if 0 <= step - offset < TILES:
+                stage(step - offset)
 
-        def on_group(step, offset, stage, size=GROUP_TILES):
-            q = group_at(step, offset, size)
-            if q is not None:
-                stage(q)
+        def on_pair(step, offset, stage):
+            pair, r = divmod(step - offset, PAIR)
+            if r == 0 and 0 <= pair < TILES // PAIR:
+                stage(pair)
 
+        group_wz(0, 0, nc.vector.tensor_copy)
+        group_wz(0, 1, nc.vector.tensor_copy)
         for step in range(STEPS):
-            if step % BATCH_TILES == 0 and step // BATCH_TILES + 2 < BATCHES:
-                load_x(step // BATCH_TILES + 2)
-            on_tile(step, AT_WORDS + 1, lambda i: words_out(i, 1, 2 if step in V_FULL else 1 if step in V_HALF else 0))
-            log_slot()
-            for j in tensor_setup.get(step - 1, ()):
-                if j not in ETA_ON_V:
+            if step % LOAD_TILES == 0 and step // LOAD_TILES + 2 < TILES // LOAD_TILES:
+                load_x(step // LOAD_TILES + 2)
+            on_tile(step, AT_WORDS + 1, lambda i: words_out(i, 1, slices_on_vector(step)))
+            series_slot()
+            for j in eta_steps.get(step - 1, ()):
+                if j not in eta_on_vector:
                     eta_out(j, nc.scalar.copy)
-            on_tile(step, AT_MAX2, lambda i: max2_turn(i, 0))
-            on_tile(step, AT_EXP2, exp2)
-            log_slot()
+            on_tile(step, AT_ROW_MAX, lambda i: turn_rows(i, 0))
+            on_tile(step, AT_ROW_SUM, row_sum)
+            series_slot()
             on_tile(step, AT_TURN_X, turn_x)
+
             on_tile(step, 0, scale_x)
-            if step in vector_setup:
-                vector_setup[step]()
-            on_group(step, AT_QUANT_X, quant_x)
-            on_group(step, AT_QUANT_C, quant_c)
-            root_step = step in root_steps
-            split = V // 2 if root_step and step < AT_EXP2 + SMALL_FROM else 0
-            if step in CATCH_UP:
-                finish_slot("vector")
+            if step in vector_prep:
+                vector_prep[step]()
+            on_pair(step, AT_QUANT_X, quant_x)
+            on_pair(step, AT_WORDS, quant_c)
+            if TILES + AT_LOGITS <= step < TILES + AT_SOFTMAX:
+                finish_slot(nc.vector, slice(0, V))
+            split = V // 2 if step in root_steps else 0
             if split:
-                finish_slot("vector", slice(0, split))
-            log_slot()
-            on_tile(step, AT_CENTRE, invert)
-            on_tile(step, AT_CENTRE, centre)
-            on_tile(step, AT_EXP2, log_root_if_last)
-            if step <= G_LAST:
-                finish_slot("gpsimd", slice(split, V))
-            for j in tensor_setup.get(step - 1, ()):
-                if j in ETA_ON_V:
+                finish_slot(nc.vector, slice(0, split))
+            series_slot()
+
+            on_tile(step, AT_INVERT, invert)
+            on_tile(step, AT_ROW_SUM, take_root)
+            if step <= TILES + AT_WORDS:
+                finish_slot(nc.gpsimd, slice(split, V))
+            for j in eta_steps.get(step - 1, ()):
+                if j in eta_on_vector:
                     eta_out(j, nc.vector.tensor_copy)
-            on_tile(step, AT_MAX2, lambda i: max2(i, 0))
+            on_tile(step, AT_ROW_MAX, lambda i: row_max(i, 0))
             on_tile(step, AT_LOGITS, logits_mm)
-            on_tile(step, AT_MAX1, max1)
+            on_tile(step, AT_SOFTMAX, turn_logits)
             on_tile(step, AT_LOGITS, logits_out)
-            log_slot()
-            on_tile(step, AT_MAX1, max1_reduce)
-            on_tile(step, AT_MAX2, lambda i: max2_turn(i, 1))
-            on_tile(step, AT_MAX2, lambda i: max2(i, 1))
-            on_tile(step, AT_MAX1, exp1)
+            series_slot()
+            on_tile(step, AT_SOFTMAX, logit_max)
+            on_tile(step, AT_ROW_MAX, lambda i: turn_rows(i, 1))
+            on_tile(step, AT_ROW_MAX, lambda i: row_max(i, 1))
+            on_tile(step, AT_SOFTMAX, logit_exp)
             on_tile(step, AT_GAIN, gain)
             on_tile(step, AT_WORDS, lambda i: words_mm(i, 0))
             on_tile(step, AT_WORDS, lambda i: words_mm(i, 1))
             on_tile(step, AT_WORDS, lambda i: words_out(i, 0, 0))
-            for j in tensor_setup.get(step, ()):
+            for j in eta_steps.get(step, ()):
                 eta_mm(j)
-            if step in scalar_setup:
-                scalar_setup[step]()
-            on_tile(step, AT_EXP2, after_exp2)
-        while chain_todo or finish_todo:
-            log_slot()
-            finish_slot("vector")
+            if step in scalar_prep:
+                scalar_prep[step]()
+            on_tile(step, AT_ROW_SUM, queue_series)
+        while series_todo or finish_todo:
+            series_slot()
+            finish_slot(nc.vector, slice(0, V))

import math
from contextlib import ExitStack

import concourse.mybir as mybir
from concourse.masks import make_identity

N, V, K, E = 4096, 1024, 512, 512
FLOPS = 2 * N * V * K + 2 * K * E * V + 2 * N * K * V

F32 = mybir.dt.float32
BF16 = mybir.dt.bfloat16
U32 = mybir.dt.uint32
U8 = mybir.dt.uint8
FP8 = mybir.dt.float8_e4m3fn
FP8X4 = mybir.dt.float8_e4m3fn_x4
ALU = mybir.AluOpType
ACT = mybir.ActivationFunctionType

P = 128
PACK = 4
BANK = 512
TILES = N // P
WORD_SLICES = V // P
LOAD_TILES = 4
PAIR = 2
PAIR_TOKENS = PAIR * P

AT_TURN_X = 1
AT_QUANT_X = 5
AT_LOGITS = 8
AT_SOFTMAX = AT_LOGITS + PAIR
AT_INVERT = AT_SOFTMAX + 1
AT_GAIN = AT_INVERT + 1
AT_WORDS = AT_GAIN + PAIR
AT_ROW_MAX = AT_WORDS + PAIR
AT_ROW_SUM = AT_ROW_MAX + 1
STEPS = TILES + AT_ROW_SUM + 1

DRAIN = TILES + 2

SMALL_BATCHES_FROM = 20
LOG_BATCHES = [(f, 4) for f in range(0, SMALL_BATCHES_FROM, 4)] + [(f, 2) for f in range(SMALL_BATCHES_FROM, TILES, 2)]
ROOT = 1024


def tile_sparseadditiveembeddedtopicdecoder_t_kernel(tc, x_bytes, x_scale, wz, bz, g, alpha, rho, m, out):
    nc = tc.nc
    with ExitStack() as ctx:
        keep = ctx.enter_context(tc.tile_pool(name="keep", bufs=1))
        work = ctx.enter_context(tc.tile_pool(name="work", bufs=2))
        psum = ctx.enter_context(tc.psum_pool(name="psum", bufs=1))
        ctx.enter_context(tc.manual_schedule())

        live = {}
        batch_of = {first + a: (b, a) for b, (first, count) in enumerate(LOG_BATCHES) for a in range(count)}

        def bank(role):
            return psum.tile([P, BANK], F32, name=role, tag=role)

        def wide_tile(shape, dtype):
            return work.tile(shape, dtype, name="wide", tag="wide", bufs=11, align_bytes=64)

        def quantise(codes, scales, grouped):
            nc.vector.quantize_mx(out=codes.bitcast(FP8X4), scales=scales, in_=grouped)

        def mx_pass(acc, lhs_codes, lhs_scales, rhs_codes, rhs_scales, start, stop):
            nc.tensor.matmul_mx(
                out=acc, lhsT=lhs_codes.bitcast(FP8X4), lhsT_scale=lhs_scales,
                rhs=rhs_codes.bitcast(FP8X4), rhs_scale=rhs_scales, start=start, stop=stop,
            )

        def load_x(q):
            xb = work.tile([P, LOAD_TILES * V], U8, name="xb", tag="xb", bufs=3)
            rows = x_bytes[q * LOAD_TILES * P:(q + 1) * LOAD_TILES * P, :]
            nc.sync.dma_start(out=xb[:], in_=rows.rearrange("(n a) v -> n (a v)", a=LOAD_TILES))
            live["xb", q] = xb

        def load_wz(h):
            raw = keep.tile([P, PACK, K], BF16, name="wz_raw%d" % h)
            nc.sync.dma_start(out=raw[:], in_=wz[h * 512:(h + 1) * 512, :].rearrange("(p t) c -> p t c", t=PACK))
            return raw

        def load_rho(half):
            raw = keep.tile([P, PACK, 512], BF16, name="rho_raw%d" % half)
            nc.sync.dma_start(out=raw[:], in_=rho.rearrange("(p t) v -> p t v", t=PACK)[:, :, half * 512:(half + 1) * 512])
            return raw

        scale_cols = keep.tile([P, 2, PACK], F32)
        nc.sync.dma_start(out=scale_cols[:], in_=x_scale.rearrange("o (h p t) -> p (o h) t", p=P, t=PACK))
        wz_raw = [load_wz(0)]
        load_x(0)
        wz_raw.append(load_wz(1))
        bz_raw = keep.tile([P, PACK], BF16)
        nc.sync.dma_start(out=bz_raw[:], in_=bz.rearrange("(p t) -> p t", t=PACK))
        g_raw = keep.tile([P, PACK], BF16)
        nc.sync.dma_start(out=g_raw[:], in_=g.rearrange("(p t) -> p t", t=PACK))
        load_x(1)
        alpha_raw = keep.tile([P, PACK, E], BF16)
        nc.sync.dma_start(out=alpha_raw[:], in_=alpha.rearrange("(r t) e -> r t e", t=PACK))
        rho_raw = [load_rho(0), load_rho(1)]

        ident = keep.tile([P, P], F32)
        make_identity(nc, ident[:])
        m_rows = keep.tile([P, P], BF16)
        nc.gpsimd.memset(m_rows[:], 0.0)
        nc.sync.dma_start(out=m_rows[0:WORD_SLICES, :], in_=m.rearrange("(j w) -> j w", w=P))

        x_scales = keep.tile([P, V], F32)
        for u in range(2):
            spread = bank("row_bank%d" % u)
            for h in range(2):
                for e in range(2):
                    col = scale_cols[:, h, 2 * u + e:2 * u + e + 1].to_broadcast([P, P])
                    nc.tensor.transpose(spread[:, (2 * h + e) * P:(2 * h + e + 1) * P], col, ident[:])
            nc.scalar.activation(
                out=x_scales[:, u * 512:(u + 1) * 512].rearrange("n (h p e) -> n h p e", h=2, e=2),
                in_=spread[:].rearrange("n (h e p) -> n h p e", h=2, e=2), func=ACT.Copy,
            )

        wz_codes = keep.tile([P, 2, K], U32, align_bytes=64)
        wz_scales = keep.tile([P, 2, K], U8, align_bytes=64)
        alpha_codes = keep.tile([P, K], U32, align_bytes=64)
        alpha_scales = keep.tile([P, K], U8, align_bytes=64)
        rho_codes = keep.tile([P, V], U32, align_bytes=64)
        rho_scales = keep.tile([P, V], U8, align_bytes=64)
        eta_codes = keep.tile([P, V], U32, align_bytes=64)
        eta_scales = keep.tile([P, V], U8, align_bytes=64)
        neg_bz_cols = keep.tile([P, PACK], F32)
        gain_cols = keep.tile([P, PACK], F32)
        gain_rows = keep.tile([P, K], F32)
        m_rows32 = keep.tile([P, P], F32)
        m_cols = keep.tile([P, WORD_SLICES], F32)
        exp_sink = keep.tile([P, V], BF16)
        root_power = keep.tile([P, LOG_BATCHES[0][1]], F32)
        nc.gpsimd.memset(root_power[:], 1.0 / ROOT)

        def group_wz(h, part, copy):
            if part == 0:
                live["wz", h] = wide_tile([P, K * PACK], BF16)
            slices = slice(2 * part, 2 * part + 2)
            copy(out=live["wz", h][:].rearrange("p (s r t) -> p s r t", s=PACK, t=PACK)[:, slices],
                 in_=wz_raw[h][:].rearrange("p t (r s) -> p s r t", s=PACK)[:, slices])

        def quant_wz(h):
            quantise(wz_codes[:, h, :], wz_scales[:, h, :], live["wz", h][:])

        def cast_vectors():
            nc.vector.tensor_scalar(out=neg_bz_cols[:], in0=bz_raw[:], scalar1=-1.0, scalar2=None, op0=ALU.mult)
            nc.vector.tensor_scalar(out=gain_cols[:], in0=g_raw[:], scalar1=float(K), scalar2=None, op0=ALU.mult)

        def spread_gain():
            nc.scalar.copy(out=gain_rows[:].rearrange("p (n t) -> p n t", t=PACK),
                           in_=gain_cols[:].unsqueeze(1).to_broadcast([P, P, PACK]))

        def turn_alpha():
            grouped = wide_tile([P, K * PACK], BF16)
            pairs = grouped[:].bitcast(F32).rearrange("p (s r u) -> p s r u", s=PACK, u=2)
            for half, role in enumerate(("logit_bank", "gain_bank")):
                turned = bank(role)
                for s in range(2):
                    words = alpha_raw[:, 2 * half + s, :].bitcast(F32)
                    for u in range(2):
                        nc.tensor.transpose(turned[:, (2 * s + u) * P:(2 * s + u + 1) * P], words[:, u:2 * P:2], ident[:])
                nc.scalar.copy(out=pairs[:, 2 * half:2 * half + 2, :, :],
                               in_=turned[:].rearrange("p (s u r) -> p s r u", s=2, u=2))
            live["alpha"] = grouped

        def quant_alpha():
            quantise(alpha_codes[:], alpha_scales[:], live["alpha"][:])

        def group_rho(half, part, copy):
            if part == 0:
                live["rho", half] = wide_tile([P, 512 * PACK], BF16)
            copy(out=live["rho", half][:, part * 1024:(part + 1) * 1024].rearrange("p (c i t) -> p c t i", i=4, t=PACK),
                 in_=rho_raw[half][:, :, part * 256:(part + 1) * 256].rearrange("p t (c i) -> p c t i", i=4))

        def quant_rho(half):
            cols = slice(half * 512, (half + 1) * 512)
            quantise(rho_codes[:, cols], rho_scales[:, cols], live["rho", half][:])

        def turn_m():
            nc.scalar.copy(out=m_rows32[:], in_=m_rows[:])
            turned = bank("gain_bank")
            nc.tensor.transpose(turned[:, 0:P], m_rows32[:], ident[:])
            nc.scalar.copy(out=m_cols[:], in_=turned[:, 0:WORD_SLICES])

        def eta_mm(j):
            acc = bank("row_bank%d" % (j % 2))
            cols = slice(j * P, (j + 1) * P)
            for t in range(PACK):
                topics = slice(t * P, (t + 1) * P)
                mx_pass(acc[:, topics], alpha_codes[:, topics], alpha_scales[:, topics],
                        rho_codes[:, cols], rho_scales[:, cols], True, True)
            live["eta_acc", j] = acc

        def eta_out(j, copy):
            half, r = divmod(j, 4)
            if r == 0:
                live["eta", half] = wide_tile([P, 512 * PACK], BF16)
            copy(out=live["eta", half][:, r * 512:(r + 1) * 512].rearrange("p (w t) -> p w t", t=PACK),
                 in_=live["eta_acc", j][:].rearrange("p (t w) -> p w t", t=PACK))

        def quant_eta(half):
            cols = slice(half * 512, (half + 1) * 512)
            quantise(eta_codes[:, cols], eta_scales[:, cols], live["eta", half][:])

        def scale_x(i):
            q, a = divmod(i, LOAD_TILES)
            xs = work.tile([P, V], BF16, name="xs", tag="xs", bufs=4)
            codes = live["xb", q][:, a * V:(a + 1) * V].bitcast(FP8)
            nc.vector.tensor_tensor(
                out=xs[:].rearrange("n (u c e) -> n u c e", u=2, e=2),
                in0=codes.rearrange("n (c u e) -> n u c e", u=2, e=2),
                in1=x_scales[:].rearrange("n (u c e) -> n u c e", u=2, e=2), op=ALU.mult,
            )
            live["xs", i] = xs

        def turn_x(i):
            pair, a = divmod(i, PAIR)
            if a == 0:
                live["xw", pair] = work.tile([P, 2, PAIR_TOKENS * PACK], BF16, name="xw", tag="xw", bufs=3, align_bytes=64)
            words = live["xs", i][:].bitcast(F32)
            turned = bank("x_bank")
            for c in range(4):
                nc.tensor.transpose(turned[:, c * P:(c + 1) * P], words[:, c * P:(c + 1) * P], ident[:])
            tokens = live["xw", pair][:].bitcast(F32).rearrange("p h (n u) -> p h n u", u=2)
            nc.scalar.copy(out=tokens[:, :, a * P:(a + 1) * P, :],
                           in_=turned[:].rearrange("p (u h n) -> p h n u", u=2, h=2))

        def quant_x(pair):
            codes = work.tile([P, 2, PAIR_TOKENS], U32, name="x_codes", tag="x_codes", bufs=4, align_bytes=64)
            scales = work.tile([P, 2, PAIR_TOKENS], U8, name="x_mx_scales", tag="x_mx_scales", bufs=4, align_bytes=64)
            quantise(codes[:].rearrange("p h n -> p (h n)"), scales[:].rearrange("p h n -> p (h n)"),
                     live["xw", pair][:].rearrange("p h n -> p (h n)"))
            live["xq", pair] = (codes, scales)

        def logits_mm(i):
            pair, a = divmod(i, PAIR)
            acc = bank("mx_bank2")
            codes, scales = live["xq", pair]
            for r in range(2):
                topics = slice((2 * a + r) * P, (2 * a + r + 1) * P)
                for h in range(2):
                    mx_pass(acc[:, r * PAIR_TOKENS:(r + 1) * PAIR_TOKENS], wz_codes[:, h, topics], wz_scales[:, h, topics],
                            codes[:, h, :], scales[:, h, :], h == 0, h == 1)
            live["logit_acc"] = acc

        def logits_out(i):
            pair, a = divmod(i, PAIR)
            for r in range(2):
                t = 2 * a + r
                neg_logits = work.tile([P, PAIR_TOKENS], F32, name="neg_logits", tag="neg_logits", bufs=8)
                nc.scalar.activation(out=neg_logits[:], in_=live["logit_acc"][:, r * PAIR_TOKENS:(r + 1) * PAIR_TOKENS],
                                     func=ACT.Identity, scale=-1.0, bias=neg_bz_cols[:, t:t + 1])
                live["neg_logits", pair, t] = neg_logits

        def turn_logits(i):
            pair, a = divmod(i, PAIR)
            turned = bank("logit_bank")
            for t in range(PACK):
                nc.tensor.transpose(turned[:, t * P:(t + 1) * P], live["neg_logits", pair, t][:, a * P:(a + 1) * P], ident[:])
            live["logit_rows", i] = turned

        def logit_max(i):
            neg_max = work.tile([P, 1], F32, name="neg_logit_max", tag="neg_logit_max", bufs=3)
            nc.vector.tensor_reduce(out=neg_max[:], in_=live["logit_rows", i][:], axis=mybir.AxisListType.X, op=ALU.min)
            live["neg_logit_max", i] = neg_max

        def logit_exp(i):
            powers = work.tile([P, K], F32, name="powers", tag="powers", bufs=4)
            total = work.tile([P, 1], F32, name="power_sum", tag="power_sum", bufs=3)
            nc.scalar.activation(out=powers[:], in_=live["logit_rows", i][:], func=ACT.Exp, scale=-1.0,
                                 bias=live["neg_logit_max", i][:], accum_out=total[:])
            live["powers", i] = powers
            live["power_sum", i] = total

        def by_diagonal(i):
            return i + AT_GAIN < DRAIN

        def invert(i):
            inv = work.tile([P, 1], F32, name="inv_sum", tag="inv_sum", bufs=3)
            nc.vector.reciprocal(out=inv[:], in_=live["power_sum", i][:])
            if by_diagonal(i):
                scaled = work.tile([P, P], F32, name="inv_diag", tag="inv_diag", bufs=3)
                source = ident
            else:
                scaled = work.tile([P, K], F32, name="theta", tag="theta", bufs=3)
                source = live["powers", i]
            nc.gpsimd.tensor_scalar(out=scaled[:], in0=source[:], scalar1=inv[:], scalar2=1.0, op0=ALU.mult, op1=ALU.mult)
            live["scaled", i] = scaled

        def gain(i):
            pair, a = divmod(i, PAIR)
            if a == 0:
                live["c", pair] = work.tile([P, PAIR_TOKENS * PACK], BF16, name="c", tag="c", bufs=2, align_bytes=64)
            c_tile = live["c", pair][:, a * K:(a + 1) * K]
            turned = bank("gain_bank")
            if by_diagonal(i):
                for t in range(PACK):
                    nc.tensor.matmul(turned[:, t:K:PACK], lhsT=live["powers", i][:, t * P:(t + 1) * P], rhs=live["scaled", i][:],
                                     start=True, stop=True)
                nc.vector.scalar_tensor_tensor(out=c_tile, in0=turned[:], scalar=-1.0 / K, in1=gain_rows[:],
                                               op0=ALU.add, op1=ALU.mult)
            else:
                for t in range(PACK):
                    nc.tensor.transpose(turned[:, t * P:(t + 1) * P], live["scaled", i][:, t * P:(t + 1) * P], ident[:])
                nc.vector.scalar_tensor_tensor(
                    out=c_tile.rearrange("p (n t) -> p n t", t=PACK), in0=turned[:].rearrange("p (t n) -> p n t", t=PACK),
                    scalar=-1.0 / K, in1=gain_cols[:].unsqueeze(1).to_broadcast([P, P, PACK]), op0=ALU.add, op1=ALU.mult,
                )

        def quant_c(pair):
            codes = work.tile([P, PAIR_TOKENS], U32, name="c_codes", tag="c_codes", bufs=2, align_bytes=64)
            scales = work.tile([P, PAIR_TOKENS], U8, name="c_mx_scales", tag="c_mx_scales", bufs=2, align_bytes=64)
            quantise(codes[:], scales[:], live["c", pair][:])
            live["cq", pair] = (codes, scales)

        def words_mm(i, b):
            pair, a = divmod(i, PAIR)
            acc = bank("mx_bank%d" % b)
            codes, scales = live["cq", pair]
            for r in range(2):
                j = 4 * a + 2 * b + r
                cols = slice(j * P, (j + 1) * P)
                mx_pass(acc[:, r * PAIR_TOKENS:(r + 1) * PAIR_TOKENS], eta_codes[:, cols], eta_scales[:, cols],
                        codes[:], scales[:], True, True)
            live["word_acc", b] = acc

        def words_out(i, b, on_vector):
            pair, a = divmod(i, PAIR)
            for r in range(2):
                j = 4 * a + 2 * b + r
                t_slice = work.tile([P, PAIR_TOKENS], F32, name="t_slice", tag="t_slice", bufs=16)
                acc = live["word_acc", b][:, r * PAIR_TOKENS:(r + 1) * PAIR_TOKENS]
                if r < on_vector:
                    nc.vector.tensor_scalar(out=t_slice[:], in0=acc, scalar1=1.0 / math.sqrt(K),
                                            scalar2=m_cols[:, j:j + 1], op0=ALU.mult, op1=ALU.add)
                else:
                    nc.scalar.activation(out=t_slice[:], in_=acc, func=ACT.Identity,
                                         scale=1.0 / math.sqrt(K), bias=m_cols[:, j:j + 1])
                live["t_slice", pair, j] = t_slice

        def batch_tile(key, b, bufs):
            columns = work.tile([P, LOG_BATCHES[b][1]], F32, name=key, tag=key, bufs=bufs)
            live[key, b] = columns
            return columns

        def turn_rows(i, half):
            pair, a = divmod(i, PAIR)
            turned = bank("row_bank%d" % half)
            for r in range(4):
                nc.tensor.transpose(turned[:, r * P:(r + 1) * P], live["t_slice", pair, 4 * half + r][:, a * P:(a + 1) * P], ident[:])
            live["t_rows", half] = turned

        def row_max(i, half):
            b, a = batch_of[i]
            if half == 0:
                live["neg_t", i] = wide_tile([P, V], F32)
                live["half_min", i] = work.tile([P, 1], F32, name="half_min", tag="half_min", bufs=2)
                if a == 0:
                    batch_tile("neg_max", b, 4)
            nc.vector.tensor_scalar(
                out=live["neg_t", i][:, half * BANK:(half + 1) * BANK], in0=live["t_rows", half][:], scalar1=-1.0,
                scalar2=None if half == 0 else live["half_min", i][:], op0=ALU.mult, op1=ALU.min,
                accum_out=live["half_min", i][:] if half == 0 else live["neg_max", b][:, a:a + 1],
            )

        def row_sum(i):
            b, a = batch_of[i]
            if a == 0:
                batch_tile("row_sums", b, 3)
            nc.scalar.activation(out=exp_sink[:], in_=live["neg_t", i][:], func=ACT.Exp, scale=-1.0,
                                 bias=live["neg_max", b][:, a:a + 1], accum_out=live["row_sums", b][:, a:a + 1])

        def log_root(b):
            nc.gpsimd.tensor_tensor(out=batch_tile("root", b, 3)[:], in0=live["row_sums", b][:],
                                    in1=root_power[:, 0:LOG_BATCHES[b][1]], op=ALU.pow)

        def log_start(b):
            root = live["root", b][:]
            centre = float(V) ** (-1.0 / ROOT)
            nc.scalar.activation(out=batch_tile("horner0", b, 3)[:], in_=root, func=ACT.Identity,
                                 scale=-centre / 4 / ROOT ** 2, bias=(1.0 / 3 + 1.0 / 4) / ROOT ** 2)
            nc.scalar.activation(out=batch_tile("w", b, 3)[:], in_=root, func=ACT.Identity, scale=-ROOT * centre, bias=float(ROOT))

        def log_step(b, src, dst, bias_of):
            result = batch_tile(dst, b, 3)
            for a in range(LOG_BATCHES[b][1]):
                nc.scalar.activation(out=result[:, a:a + 1], in_=live[src, b][:, a:a + 1], func=ACT.Identity,
                                     scale=live["w", b][:, a:a + 1], bias=bias_of(a))

        series = [
            log_start,
            lambda b: log_step(b, "horner0", "horner1", lambda a: 0.5 / ROOT),
            lambda b: log_step(b, "horner1", "horner2", lambda a: 1.0),
            lambda b: log_step(b, "horner2", "shift", lambda a: live["neg_max", b][:, a:a + 1]),
        ]
        series_todo = []
        finish_todo = []

        def closes_batch(i):
            b, a = batch_of[i]
            return a == LOG_BATCHES[b][1] - 1

        def take_root(i):
            if closes_batch(i):
                log_root(batch_of[i][0])

        def queue_series(i):
            if closes_batch(i):
                series_todo.extend((batch_of[i][0], link) for link in range(len(series)))

        def series_slot():
            if series_todo:
                b, link = series_todo.pop(0)
                series[link](b)
                if link == len(series) - 1:
                    first, count = LOG_BATCHES[b]
                    finish_todo.extend(range(first, first + count))

        def finish_slot(engine, cols):
            if finish_todo:
                i = finish_todo[0]
                b, a = batch_of[i]
                part = live["neg_t", i][:, cols]
                engine.tensor_scalar(out=part, in0=part, scalar1=-1.0, scalar2=live["shift", b][:, a:a + 1],
                                     op0=ALU.mult, op1=ALU.add)
                if cols.stop == V:
                    q, a = divmod(finish_todo.pop(0), LOAD_TILES)
                    rows = out[q * LOAD_TILES * P:(q + 1) * LOAD_TILES * P, :].rearrange("(n a) v -> n a v", a=LOAD_TILES)
                    nc.sync.dma_start(out=rows[:, a, :], in_=live["neg_t", i][:])

        vector_prep = {
            1: cast_vectors, 2: lambda: quant_wz(0), 3: lambda: quant_wz(1), 4: quant_alpha,
            6: lambda: (quant_rho(0), group_rho(1, 1, nc.vector.tensor_copy)), 7: lambda: quant_rho(1),
            AT_SOFTMAX: lambda: quant_eta(0), AT_WORDS: lambda: quant_eta(1),
        }
        scalar_prep = {
            0: lambda: group_wz(1, 0, nc.scalar.copy), 1: lambda: group_wz(1, 1, nc.scalar.copy), 2: turn_alpha,
            3: lambda: group_rho(0, 0, nc.scalar.copy), 4: lambda: group_rho(0, 1, nc.scalar.copy),
            5: lambda: group_rho(1, 0, nc.scalar.copy), 6: turn_m, 7: spread_gain,
        }
        eta_steps = {7: (0, 1), 8: (2, 3), 9: (4, 5), 10: (6,), 11: (7,)}
        eta_on_vector = (3, 5)
        root_steps = [AT_ROW_SUM + first + count - 1 for first, count in LOG_BATCHES if count == 4]

        def slices_on_vector(step):
            if step >= TILES + AT_GAIN:
                return 2
            return 1 if DRAIN <= step < TILES + AT_LOGITS or step - 1 in root_steps else 0

        def on_tile(step, offset, stage):
            if 0 <= step - offset < TILES:
                stage(step - offset)

        def on_pair(step, offset, stage):
            pair, r = divmod(step - offset, PAIR)
            if r == 0 and 0 <= pair < TILES // PAIR:
                stage(pair)

        group_wz(0, 0, nc.vector.tensor_copy)
        group_wz(0, 1, nc.vector.tensor_copy)
        for step in range(STEPS):
            if step % LOAD_TILES == 0 and step // LOAD_TILES + 2 < TILES // LOAD_TILES:
                load_x(step // LOAD_TILES + 2)
            on_tile(step, AT_WORDS + 1, lambda i: words_out(i, 1, slices_on_vector(step)))
            series_slot()
            for j in eta_steps.get(step - 1, ()):
                if j not in eta_on_vector:
                    eta_out(j, nc.scalar.copy)
            on_tile(step, AT_ROW_MAX, lambda i: turn_rows(i, 0))
            on_tile(step, AT_ROW_SUM, row_sum)
            series_slot()
            on_tile(step, AT_TURN_X, turn_x)

            on_tile(step, 0, scale_x)
            if step in vector_prep:
                vector_prep[step]()
            on_pair(step, AT_QUANT_X, quant_x)
            on_pair(step, AT_WORDS, quant_c)
            if TILES + AT_LOGITS <= step < TILES + AT_SOFTMAX:
                finish_slot(nc.vector, slice(0, V))
            split = V // 2 if step in root_steps else 0
            if split:
                finish_slot(nc.vector, slice(0, split))
            series_slot()

            on_tile(step, AT_INVERT, invert)
            on_tile(step, AT_ROW_SUM, take_root)
            if step <= TILES + AT_WORDS:
                finish_slot(nc.gpsimd, slice(split, V))
            for j in eta_steps.get(step - 1, ()):
                if j in eta_on_vector:
                    eta_out(j, nc.vector.tensor_copy)
            on_tile(step, AT_ROW_MAX, lambda i: row_max(i, 0))
            on_tile(step, AT_LOGITS, logits_mm)
            on_tile(step, AT_SOFTMAX, turn_logits)
            on_tile(step, AT_LOGITS, logits_out)
            series_slot()
            on_tile(step, AT_SOFTMAX, logit_max)
            on_tile(step, AT_ROW_MAX, lambda i: turn_rows(i, 1))
            on_tile(step, AT_ROW_MAX, lambda i: row_max(i, 1))
            on_tile(step, AT_SOFTMAX, logit_exp)
            on_tile(step, AT_GAIN, gain)
            on_tile(step, AT_WORDS, lambda i: words_mm(i, 0))
            on_tile(step, AT_WORDS, lambda i: words_mm(i, 1))
            on_tile(step, AT_WORDS, lambda i: words_out(i, 0, 0))
            for j in eta_steps.get(step, ()):
                eta_mm(j)
            if step in scalar_prep:
                scalar_prep[step]()
            on_tile(step, AT_ROW_SUM, queue_series)
        while series_todo or finish_todo:
            series_slot()
            finish_slot(nc.vector, slice(0, V))
